import numpy as np
import ml_dtypes


def mxq(x, axis, fmt="e4m3"):
    dtype, down = {"e4m3": (ml_dtypes.float8_e4m3fn, 7), "e5m2": (ml_dtypes.float8_e5m2, 14)}[fmt]
    v = np.moveaxis(np.asarray(x, np.float32).astype(ml_dtypes.bfloat16).astype(np.float64), axis, -1)
    blocks = v.reshape(v.shape[:-1] + (-1, 32))
    amax = np.abs(blocks).max(-1, keepdims=True)
    byte = np.maximum(np.where(amax > 0, np.frexp(amax)[1] - 1 + 127, 0) - down, 1)
    scale = np.exp2(byte - 127.0)
    codes = (blocks / scale).astype(np.float32).astype(dtype).astype(np.float64)
    return np.moveaxis((codes * scale).reshape(v.shape), -1, axis)


WIDE = False


def mx_kscale(k):
    if not WIDE:
        return np.ones(k)
    levels = np.array([10, -10, 5, -5, 0])
    if k % 512:
        return np.exp2(np.random.permutation(np.resize(levels, k // 32))).repeat(32)
    a = np.empty((k // 512, 16))
    for p in range(k // 512):
        a[p, :8] = np.random.permutation(np.resize(levels, 8))
        for g in range(8):
            far = levels[np.abs(levels - a[p, g]) >= 10]
            a[p, g + 8] = far[np.random.randint(len(far))]
    return np.exp2(a.ravel()).repeat(32)


def f64(x):
    return np.asarray(x).astype(np.float64)


def striped(idx):
    return np.tile(idx.reshape(-1, 16).T, (8, 1)).astype(np.uint16)


def unstriped(offs):
    return offs[:16].T.reshape(-1).astype(np.int64)


def pack_weight(w):
    k, n = w.shape
    w = f64(np.asarray(w, np.float32).astype(ml_dtypes.bfloat16)).reshape(k // 32, 32, n)
    amax = np.abs(w).max(1)
    byte = np.clip(np.where(amax > 0, np.frexp(amax)[1] - 1 + 127 - 7, 1), 1, 254)
    scaled = (w * np.exp2(127.0 - byte)[:, None, :]).reshape(k, n).astype(np.float32)
    words = np.ascontiguousarray(scaled.reshape(k // 512, 128, 4, n).transpose(0, 1, 3, 2)).astype(ml_dtypes.float8_e4m3fn).view(np.uint8)
    return words, np.ascontiguousarray(byte.astype(np.uint8).reshape(k // 512, 16, n))


def unpack_weight(words, scales):
    g, p, n, _ = words.shape
    vals = np.ascontiguousarray(words).view(ml_dtypes.float8_e4m3fn).astype(np.float64) * np.repeat(np.exp2(scales.astype(np.float64) - 127.0), 8, axis=1)[..., None]
    return vals.transpose(0, 1, 3, 2).reshape(g * 512, n)


E2M1 = np.array([0.0, 0.5, 1.0, 1.5, 2.0, 3.0, 4.0, 6.0, -0.0, -0.5, -1.0, -1.5, -2.0, -3.0, -4.0, -6.0])


def pack_fp4(w):
    k, n = w.shape
    w = f64(np.asarray(w, np.float32).astype(ml_dtypes.bfloat16)).reshape(k // 32, 32, n)
    amax = np.abs(w).max(1)
    mant, ex = np.frexp(amax / 6.0)
    byte = np.clip(np.where(amax > 0, np.where(mant > 0.5, ex, ex - 1) + 127, 1), 1, 254)
    scaled = (w * np.exp2(127.0 - byte)[:, None, :]).reshape(k, n).astype(np.float32)
    c = np.ascontiguousarray(scaled.reshape(k // 512, 128, 4, n).transpose(0, 1, 3, 2)).astype(ml_dtypes.float4_e2m1fn).view(np.uint8) & 0xF
    words = (c[..., 0::2] | (c[..., 1::2] << 4)).reshape(k // 512, 128, 2 * n)
    return np.ascontiguousarray(words), np.ascontiguousarray(byte.astype(np.uint8).reshape(k // 512, 16, n))


def unpack_fp4(words, scales):
    g, _, n = scales.shape
    words = np.ascontiguousarray(words).reshape(g, 128, n, 2)
    nib = np.empty((g, 128, n, 4), np.uint8)
    nib[..., 0::2] = words & 0xF
    nib[..., 1::2] = words >> 4
    vals = E2M1[nib] * np.repeat(np.exp2(scales.astype(np.float64) - 127.0), 8, axis=1)[..., None]
    return vals.transpose(0, 1, 3, 2).reshape(g * 512, n)


K, T, S, N, H = 512, 1024, 512, 256, 512


def setup_inputs():
    n = np.random.standard_normal
    s = mx_kscale(K)[:, None]
    u = mx_kscale(H)
    packed_xT = pack_weight(n((K, T)) * s)
    packed_w1 = pack_fp4(n((K, H)) / np.sqrt(K) / s)
    packed_w2 = pack_fp4(n((K, H)) / np.sqrt(K) / s)
    packed_w3 = pack_fp4(n((H, N)) / np.sqrt(H) / u[:, None])
    return {
        "x_words": packed_xT[0],
        "x_scales": packed_xT[1],
        "w1_words": packed_w1[0],
        "w1_scales": packed_w1[1],
        "w2_words": packed_w2[0],
        "w2_scales": packed_w2[1],
        "dec": (np.random.uniform(0.2, 1.0, (H, S))).astype(np.float32),
        "inh": (np.random.uniform(0.2, 0.8, (H, S))).astype(np.float32),
        "unit": (np.random.uniform(0.6, 1.4, (H, 1)) * u[:, None]).astype(np.float32),
        "w3_words": packed_w3[0],
        "w3_scales": packed_w3[1],
        "offs": striped(np.random.permutation(T)[:S]),
        "par": striped(np.random.permutation(S)),
        "sib": striped(np.random.permutation(S)),
    }


def reference(x_words, x_scales, w1_words, w1_scales, w2_words, w2_scales, dec, inh, unit, w3_words, w3_scales, offs, par, sib):
    xq = unpack_weight(x_words, x_scales)[:, unstriped(offs)]
    zz1 = unpack_fp4(w2_words, w2_scales).T @ xq
    exc = np.log(np.exp(zz1) + 1.0)
    ep = exc[:, unstriped(par)]
    trig = ep * f64(dec)
    y = unpack_fp4(w1_words, w1_scales).T @ xq
    base = np.log(np.exp(y) + 1.0) + 0.2
    branch = trig / (base + trig + 0.1)
    zs = zz1[:, unstriped(sib)]
    inhb = zs * f64(inh)
    llam = np.log(np.exp(np.tanh(base + trig - inhb)) + 0.5)
    hid = f64(unit) * (branch * llam + 0.4 * inhb)
    return unpack_fp4(w3_words, w3_scales).T @ mxq(hid, 0, "e4m3")

@@ -1,0 +1,234 @@
+import math
+from contextlib import ExitStack
+
+import concourse.mybir as mybir
+
+K, T, S, N, H = 512, 1024, 512, 256, 512
+FLOPS = 2 * K * S * H * 2 + 2 * H * S * N
+
+F32 = mybir.dt.float32
+BF16 = mybir.dt.bfloat16
+I32 = mybir.dt.int32
+U32 = mybir.dt.uint32
+U16 = mybir.dt.uint16
+U8 = mybir.dt.uint8
+FP8X4 = mybir.dt.float8_e4m3fn_x4
+FP4X4 = mybir.dt.float4_e2m1fn_x4
+ALU = mybir.AluOpType
+ACT = mybir.ActivationFunctionType
+
+P = 128
+PACK = 4
+SPARE = 32
+TINY = 2.0 ** -46
+CHUNK = 256
+
+
+def tile_picked_ylearnh_br_p_kernel(
+    tc, x_words, x_scales, w1_words, w1_scales, w2_words, w2_scales, dec, inh, unit, w3_words, w3_scales, offs, par, sib, out
+):
+    nc = tc.nc
+    with ExitStack() as ctx:
+        keep = ctx.enter_context(tc.tile_pool(name="keep", bufs=1))
+        psum = ctx.enter_context(tc.psum_pool(name="psum", bufs=1))
+
+        def sb(name, shape, dtype=F32):
+            return keep.tile(shape, dtype, name=name, align_bytes=64)
+
+        def load_scales(queue, plane, scales):
+            for q in range(4):
+                queue.dma_start(out=plane[32 * q : 32 * q + 4, :].bitcast(I32), in_=scales[0, 4 * q : 4 * q + 4, :].bitcast(I32))
+
+        offs_t = keep.tile([P, S // 16], U16, name="offs_t")
+        par_t = keep.tile([P, S // 16], U16, name="par_t")
+        sib_t = keep.tile([P, S // 16], U16, name="sib_t")
+        xw = sb("xw", [P, T], I32)
+        xs = sb("xs", [P, T], U8)
+        w1w, w2w, w3w = sb("w1w", [P, 2 * H], U8), sb("w2w", [P, 2 * H], U8), sb("w3w", [P, 2 * N], U8)
+        w1s, w2s, w3s = sb("w1s", [P, H], U8), sb("w2s", [P, H], U8), sb("w3s", [P, N], U8)
+        dec_t, inh_t = sb("dec_t", [P, PACK, S]), sb("inh_t", [P, PACK, S])
+        unit_t = sb("unit_t", [P, PACK])
+        zw = [sb("zw%d" % t, [P, S + SPARE]) for t in range(PACK)]
+        exc = [sb("exc%d" % t, [P, S + SPARE]) for t in range(PACK)]
+
+        nc.vector.memset(xs[:].bitcast(I32), 0)
+        for plane in (w2s, w1s, w3s):
+            nc.gpsimd.memset(plane[:].bitcast(I32), 0)
+        for window in zw + exc:
+            nc.gpsimd.memset(window[:, S:], 0.0)
+
+        nc.sync.dma_start(out=offs_t[:], in_=offs)
+        nc.sync.dma_start(out=xw[:], in_=x_words[0].rearrange("p n t -> p (n t)").bitcast(I32))
+        nc.sync.dma_start(out=w2w[:].bitcast(I32), in_=w2_words[0].bitcast(I32))
+        load_scales(nc.scalar, xs, x_scales)
+        nc.sync.dma_start(out=w1w[:].bitcast(I32), in_=w1_words[0].bitcast(I32))
+        load_scales(nc.sync, w2s, w2_scales)
+        load_scales(nc.sync, w1s, w1_scales)
+        nc.sync.dma_start(out=sib_t[:], in_=sib)
+        nc.sync.dma_start(out=inh_t[:], in_=inh.rearrange("(p t) j -> p t j", t=PACK))
+        nc.sync.dma_start(out=par_t[:], in_=par)
+        nc.sync.dma_start(out=dec_t[:], in_=dec.rearrange("(p t) j -> p t j", t=PACK))
+        nc.sync.dma_start(out=unit_t[:], in_=unit.rearrange("(p t) o -> p (t o)", t=PACK))
+        nc.sync.dma_start(out=w3w[:].bitcast(I32), in_=w3_words[0].bitcast(I32))
+        load_scales(nc.sync, w3s, w3_scales)
+
+        xg = sb("xg", [P, S], U32)
+        xgs = sb("xgs", [P, S], U8)
+        w1d, w2d = sb("w1d", [P, 2 * H], U8), sb("w2d", [P, 2 * H], U8)
+        w1sd, w2sd = sb("w1sd", [P, H], U8), sb("w2sd", [P, H], U8)
+
+        def deal_words(dst, src):
+            nc.vector.tensor_copy(
+                out=dst[:].rearrange("p (t m b) -> p t m b", t=PACK, b=2),
+                in_=src[:].rearrange("p (m t b) -> p t m b", t=PACK, b=2),
+            )
+
+        def deal_scales(dst, src):
+            nc.vector.tensor_copy(out=dst[:].rearrange("p (t m) -> p t m", t=PACK), in_=src[:].rearrange("p (m t) -> p t m", t=PACK))
+
+        deal_words(w2d, w2w)
+        nc.vector.tensor_copy(out=xgs[:], in_=xs[:].indirect(offs_t[:]))
+        nc.vector.tensor_copy(out=xg[:], in_=xw[:].bitcast(U32).indirect(offs_t[:]))
+        deal_scales(w2sd, w2s)
+        deal_words(w1d, w1w)
+        deal_scales(w1sd, w1s)
+
+        def product(bank, words, scales, t):
+            nc.tensor.matmul_mx(
+                out=bank[:],
+                lhsT=words[:, 2 * P * t : 2 * P * (t + 1)].bitcast(FP4X4),
+                lhsT_scale=scales[:, P * t : P * (t + 1)],
+                rhs=xg[:].bitcast(FP8X4),
+                rhs_scale=xgs[:],
+                start=True,
+                stop=True,
+            )
+
+        zb = [psum.tile([P, S], F32, name="zb%d" % t, tag="zb%d" % t) for t in range(PACK)]
+        yb = [psum.tile([P, S], F32, name="yb%d" % t, tag="yb%d" % t) for t in range(PACK)]
+        for t in range(PACK):
+            product(zb[t], w2d, w2sd, t)
+        for t in range(PACK):
+            product(yb[t], w1d, w1sd, t)
+
+        neg4u, u04 = sb("neg4u", [P, PACK]), sb("u04", [P, PACK])
+        nc.gpsimd.tensor_scalar(neg4u[:], unit_t[:], -4.0, 0.0, ALU.mult, ALU.add)
+        nc.gpsimd.tensor_scalar(u04[:], unit_t[:], 0.4, 0.0, ALU.mult, ALU.add)
+
+        consts = sb("consts", [P, 4])
+        nc.gpsimd.memset(consts[:], 0.0)
+        for col, value in ((1, TINY), (2, 0.2), (3, -math.log(2.0))):
+            nc.gpsimd.tensor_scalar(consts[:, col : col + 1], consts[:, 0:1], 1.0, value, ALU.mult, ALU.add)
+
+        def phase_biases(n):
+            biases = keep.tile([P, 4], F32, name="biases%d" % n, tag="biases")
+            if n == 0:
+                nc.gpsimd.tensor_copy(biases[:], consts[:])
+            else:
+                nc.scalar.copy(biases[:], consts[:])
+            return {"zero": biases[:, 0:1], "tiny": biases[:, 1:2], "fifth": biases[:, 2:3], "half": biases[:, 3:4]}
+
+        b = phase_biases(0)
+        sz, sy = sb("sz", [P, PACK, S]), sb("sy", [P, PACK, S])
+        nz, ny = sb("nz", [P, PACK, S]), sb("ny", [P, PACK, S])
+        for t in range(PACK):
+            nc.scalar.activation(sz[:, t, :], zb[t][:], ACT.Sigmoid, scale=-1.0, bias=b["zero"])
+        for t in range(PACK):
+            nc.scalar.activation(sy[:, t, :], yb[t][:], ACT.Sigmoid, scale=-1.0, bias=b["zero"])
+
+        inhb, trig = sb("inhb", [P, PACK, S]), sb("trig", [P, PACK, S])
+        for t in range(PACK):
+            nc.vector.tensor_copy(out=zw[t][:, :S], in_=zb[t][:])
+        for t in range(PACK):
+            nc.vector.tensor_tensor(inhb[:, t, :], zw[t][:].indirect(sib_t[:]), inh_t[:, t, :], ALU.mult)
+
+        b = phase_biases(1)
+        for t in range(PACK):
+            nc.scalar.activation(nz[:, t, :], sz[:, t, :], ACT.Ln, bias=b["tiny"])
+            nc.scalar.activation(ny[:, t, :], sy[:, t, :], ACT.Ln, bias=b["tiny"])
+
+        soft, dsum, arg = sb("soft", [P, PACK, S]), sb("dsum", [P, PACK, S]), sb("arg", [P, PACK, S])
+        lden, rden = sb("lden", [P, PACK, S]), sb("rden", [P, PACK, S])
+        th, sg, nll = sb("th", [P, PACK, S]), sb("sg", [P, PACK, S]), sb("nll", [P, PACK, S])
+        share, inhu, prod = sb("share", [P, PACK, S]), sb("inhu", [P, PACK, S]), sb("prod", [P, PACK, S])
+        hb = sb("hb", [P, S, PACK], BF16)
+        hq, hs = sb("hq", [P, S], U32), sb("hs", [P, S], U8)
+
+        def excite(t):
+            nc.vector.scalar_tensor_tensor(exc[t][:, :S], nz[:, t, :], -1.0, zb[t][:], ALU.mult, ALU.max)
+            nc.vector.scalar_tensor_tensor(soft[:, t, :], ny[:, t, :], -1.0, yb[t][:], ALU.mult, ALU.max)
+            nc.vector.tensor_tensor(trig[:, t, :], exc[t][:].indirect(par_t[:]), dec_t[:, t, :], ALU.mult)
+            nc.vector.tensor_tensor(dsum[:, t, :], soft[:, t, :], trig[:, t, :], ALU.add)
+
+        def log_den(t, b):
+            nc.scalar.activation(lden[:, t, :], dsum[:, t, :], ACT.Ln, scale=4.0, bias=b["fifth"])
+
+        def squash(rows, b):
+            nc.scalar.activation(th[:, rows, :], arg[:, rows, :], ACT.Tanh, bias=b["fifth"])
+            nc.scalar.activation(rden[:, rows, :], lden[:, rows, :], ACT.Sigmoid, scale=-1.0, bias=b["zero"])
+            nc.scalar.activation(sg[:, rows, :], th[:, rows, :], ACT.Sigmoid, scale=-1.0, bias=b["half"])
+
+        def scale_rows(t):
+            nc.vector.scalar_tensor_tensor(share[:, t, :], rden[:, t, :], neg4u[:, t : t + 1], trig[:, t, :], ALU.mult, ALU.mult)
+            nc.vector.tensor_scalar(inhu[:, t, :], inhb[:, t, :], u04[:, t : t + 1], None, ALU.mult)
+
+        def log_lam(rows, cols, b):
+            nc.scalar.activation(nll[:, rows, cols], sg[:, rows, cols], ACT.Ln, scale=2.0, bias=b["zero"])
+
+        def multiply(rows, cols):
+            nc.vector.tensor_tensor(prod[:, rows, cols], share[:, rows, cols], nll[:, rows, cols], ALU.mult)
+
+        def finish(rows, cols):
+            nc.vector.tensor_tensor(
+                hb[:, cols, rows].rearrange("p (c i) t -> p c t i", i=4),
+                prod[:, rows, cols].rearrange("p t (c i) -> p c t i", i=4),
+                inhu[:, rows, cols].rearrange("p t (c i) -> p c t i", i=4),
+                ALU.add,
+            )
+
+        first, second = slice(0, 2), slice(2, 4)
+        every = slice(0, S)
+        chunks = [slice(c, c + CHUNK) for c in range(0, S, CHUNK)]
+
+        for t in (0, 1):
+            excite(t)
+            log_den(t, b)
+        nc.vector.tensor_tensor(arg[:, first, :], dsum[:, first, :], inhb[:, first, :], ALU.subtract)
+        squash(first, phase_biases(2))
+        b = phase_biases(3)
+        for t in (2, 3):
+            excite(t)
+            log_den(t, b)
+        nc.vector.tensor_tensor(arg[:, second, :], dsum[:, second, :], inhb[:, second, :], ALU.subtract)
+        log_lam(first, every, b)
+        squash(second, phase_biases(4))
+        for t in (0, 1):
+            scale_rows(t)
+        multiply(first, every)
+        finish(first, every)
+        for t in (2, 3):
+            scale_rows(t)
+        b = phase_biases(5)
+        for cols in chunks:
+            log_lam(second, cols, b)
+        for cols in chunks:
+            multiply(second, cols)
+        for cols in chunks:
+            finish(second, cols)
+        for c, cols in enumerate(chunks):
+            nc.vector.quantize_mx(out=hq[:, cols].bitcast(FP8X4), scales=hs[:, cols], in_=hb[:, cols, :].rearrange("p j t -> p (j t)"))
+        for c, cols in enumerate(chunks):
+            ob = psum.tile([P, N // P, CHUNK], F32, name="ob%d" % c, tag="zb%d" % c)
+            for m in range(N // P):
+                nc.tensor.matmul_mx(
+                    out=ob[:, m, :],
+                    lhsT=w3w[:, 2 * P * m : 2 * P * (m + 1)].bitcast(FP4X4),
+                    lhsT_scale=w3s[:, P * m : P * (m + 1)],
+                    rhs=hq[:, cols].bitcast(FP8X4),
+                    rhs_scale=hs[:, cols],
+                    start=True,
+                    stop=True,
+                )
+            res = sb("res%d" % c, [P, N // P, CHUNK])
+            nc.scalar.copy(res[:], ob[:])
+            nc.sync.dma_start(out=out[:, cols].rearrange("(m p) j -> p m j", p=P), in_=res[:])

@@ -21,7 +21,6 @@ P = 128
 PACK = 4
 SPARE = 32
 TINY = 2.0 ** -46
-CHUNK = 256
 
 
 def tile_picked_ylearnh_br_p_kernel(
@@ -51,18 +50,22 @@ def tile_picked_ylearnh_br_p_kernel(
         zw = [sb("zw%d" % t, [P, S + SPARE]) for t in range(PACK)]
         exc = [sb("exc%d" % t, [P, S + SPARE]) for t in range(PACK)]
 
-        nc.vector.memset(xs[:].bitcast(I32), 0)
-        for plane in (w2s, w1s, w3s):
+        for plane in (xs, w2s, w1s, w3s):
             nc.gpsimd.memset(plane[:].bitcast(I32), 0)
+        consts = sb("consts", [P, 4])
+        nc.gpsimd.memset(consts[:], 0.0)
+        for col, value in ((1, TINY), (2, 0.2), (3, -math.log(2.0))):
+            nc.gpsimd.tensor_scalar(consts[:, col : col + 1], consts[:, 0:1], 1.0, value, ALU.mult, ALU.add)
+
         for window in zw + exc:
             nc.gpsimd.memset(window[:, S:], 0.0)
 
         nc.sync.dma_start(out=offs_t[:], in_=offs)
-        nc.sync.dma_start(out=xw[:], in_=x_words[0].rearrange("p n t -> p (n t)").bitcast(I32))
         nc.sync.dma_start(out=w2w[:].bitcast(I32), in_=w2_words[0].bitcast(I32))
-        load_scales(nc.scalar, xs, x_scales)
-        nc.sync.dma_start(out=w1w[:].bitcast(I32), in_=w1_words[0].bitcast(I32))
+        nc.scalar.dma_start(out=xw[:], in_=x_words[0].rearrange("p n t -> p (n t)").bitcast(I32))
+        load_scales(nc.sync, xs, x_scales)
         load_scales(nc.sync, w2s, w2_scales)
+        nc.sync.dma_start(out=w1w[:].bitcast(I32), in_=w1_words[0].bitcast(I32))
         load_scales(nc.sync, w1s, w1_scales)
         nc.sync.dma_start(out=sib_t[:], in_=sib)
         nc.sync.dma_start(out=inh_t[:], in_=inh.rearrange("(p t) j -> p t j", t=PACK))
@@ -86,39 +89,38 @@ def tile_picked_ylearnh_br_p_kernel(
         def deal_scales(dst, src):
             nc.vector.tensor_copy(out=dst[:].rearrange("p (t m) -> p t m", t=PACK), in_=src[:].rearrange("p (m t) -> p t m", t=PACK))
 
+        halves = [slice(0, S // 2), slice(S // 2, S)]
+        every = slice(0, S)
+
+        def pick(cols):
+            entries = offs_t[:, cols.start // 16 : cols.stop // 16]
+            nc.vector.tensor_copy(out=xgs[:, cols], in_=xs[:].indirect(entries))
+            nc.vector.tensor_copy(out=xg[:, cols], in_=xw[:].bitcast(U32).indirect(entries))
+
         deal_words(w2d, w2w)
-        nc.vector.tensor_copy(out=xgs[:], in_=xs[:].indirect(offs_t[:]))
-        nc.vector.tensor_copy(out=xg[:], in_=xw[:].bitcast(U32).indirect(offs_t[:]))
+        pick(halves[0])
         deal_scales(w2sd, w2s)
+        pick(halves[1])
         deal_words(w1d, w1w)
         deal_scales(w1sd, w1s)
 
-        def product(bank, words, scales, t):
+        def product(bank, words, scales, t, cols):
             nc.tensor.matmul_mx(
-                out=bank[:],
+                out=bank[:, cols],
                 lhsT=words[:, 2 * P * t : 2 * P * (t + 1)].bitcast(FP4X4),
                 lhsT_scale=scales[:, P * t : P * (t + 1)],
-                rhs=xg[:].bitcast(FP8X4),
-                rhs_scale=xgs[:],
+                rhs=xg[:, cols].bitcast(FP8X4),
+                rhs_scale=xgs[:, cols],
                 start=True,
                 stop=True,
             )
 
         zb = [psum.tile([P, S], F32, name="zb%d" % t, tag="zb%d" % t) for t in range(PACK)]
         yb = [psum.tile([P, S], F32, name="yb%d" % t, tag="yb%d" % t) for t in range(PACK)]
-        for t in range(PACK):
-            product(zb[t], w2d, w2sd, t)
-        for t in range(PACK):
-            product(yb[t], w1d, w1sd, t)
 
         neg4u, u04 = sb("neg4u", [P, PACK]), sb("u04", [P, PACK])
         nc.gpsimd.tensor_scalar(neg4u[:], unit_t[:], -4.0, 0.0, ALU.mult, ALU.add)
         nc.gpsimd.tensor_scalar(u04[:], unit_t[:], 0.4, 0.0, ALU.mult, ALU.add)
-
-        consts = sb("consts", [P, 4])
-        nc.gpsimd.memset(consts[:], 0.0)
-        for col, value in ((1, TINY), (2, 0.2), (3, -math.log(2.0))):
-            nc.gpsimd.tensor_scalar(consts[:, col : col + 1], consts[:, 0:1], 1.0, value, ALU.mult, ALU.add)
 
         def phase_biases(n):
             biases = keep.tile([P, 4], F32, name="biases%d" % n, tag="biases")
@@ -128,26 +130,37 @@ def tile_picked_ylearnh_br_p_kernel(
                 nc.scalar.copy(biases[:], consts[:])
             return {"zero": biases[:, 0:1], "tiny": biases[:, 1:2], "fifth": biases[:, 2:3], "half": biases[:, 3:4]}
 
+        warm = sb("warm", [P, 1])
+        nc.scalar.activation(warm[:], consts[:, 0:1], ACT.Sigmoid)
         b = phase_biases(0)
         sz, sy = sb("sz", [P, PACK, S]), sb("sy", [P, PACK, S])
         nz, ny = sb("nz", [P, PACK, S]), sb("ny", [P, PACK, S])
+        for cols in halves:
+            for t in range(PACK):
+                product(zb[t], w2d, w2sd, t, cols)
+                nc.scalar.activation(sz[:, t, cols], zb[t][:, cols], ACT.Sigmoid, scale=-1.0, bias=b["zero"])
         for t in range(PACK):
-            nc.scalar.activation(sz[:, t, :], zb[t][:], ACT.Sigmoid, scale=-1.0, bias=b["zero"])
-        for t in range(PACK):
+            product(yb[t], w1d, w1sd, t, every)
             nc.scalar.activation(sy[:, t, :], yb[t][:], ACT.Sigmoid, scale=-1.0, bias=b["zero"])
 
-        inhb, trig = sb("inhb", [P, PACK, S]), sb("trig", [P, PACK, S])
+        trig = sb("trig", [P, PACK, S])
+        inhb = [sb("inhb0", [P, 2, S])]
+        soft = [sb("soft0", [P, 2, S]), keep.tile([P, 2, S], F32, name="soft1", tag="late")]
+
+        def inhibit(t):
+            nc.vector.tensor_tensor(inhb[t // 2][:, t % 2, :], zw[t][:].indirect(sib_t[:]), inh_t[:, t, :], ALU.mult)
+
         for t in range(PACK):
             nc.vector.tensor_copy(out=zw[t][:, :S], in_=zb[t][:])
-        for t in range(PACK):
-            nc.vector.tensor_tensor(inhb[:, t, :], zw[t][:].indirect(sib_t[:]), inh_t[:, t, :], ALU.mult)
+        for t in (0, 1):
+            inhibit(t)
 
         b = phase_biases(1)
         for t in range(PACK):
             nc.scalar.activation(nz[:, t, :], sz[:, t, :], ACT.Ln, bias=b["tiny"])
             nc.scalar.activation(ny[:, t, :], sy[:, t, :], ACT.Ln, bias=b["tiny"])
 
-        soft, dsum, arg = sb("soft", [P, PACK, S]), sb("dsum", [P, PACK, S]), sb("arg", [P, PACK, S])
+        dsum, arg = sb("dsum", [P, PACK, S]), sb("arg", [P, PACK, S])
         lden, rden = sb("lden", [P, PACK, S]), sb("rden", [P, PACK, S])
         th, sg, nll = sb("th", [P, PACK, S]), sb("sg", [P, PACK, S]), sb("nll", [P, PACK, S])
         share, inhu, prod = sb("share", [P, PACK, S]), sb("inhu", [P, PACK, S]), sb("prod", [P, PACK, S])
@@ -156,21 +169,28 @@ def tile_picked_ylearnh_br_p_kernel(
 
         def excite(t):
             nc.vector.scalar_tensor_tensor(exc[t][:, :S], nz[:, t, :], -1.0, zb[t][:], ALU.mult, ALU.max)
-            nc.vector.scalar_tensor_tensor(soft[:, t, :], ny[:, t, :], -1.0, yb[t][:], ALU.mult, ALU.max)
+            nc.vector.scalar_tensor_tensor(soft[t // 2][:, t % 2, :], ny[:, t, :], -1.0, yb[t][:], ALU.mult, ALU.max)
             nc.vector.tensor_tensor(trig[:, t, :], exc[t][:].indirect(par_t[:]), dec_t[:, t, :], ALU.mult)
-            nc.vector.tensor_tensor(dsum[:, t, :], soft[:, t, :], trig[:, t, :], ALU.add)
+            nc.vector.tensor_tensor(dsum[:, t, :], soft[t // 2][:, t % 2, :], trig[:, t, :], ALU.add)
 
         def log_den(t, b):
             nc.scalar.activation(lden[:, t, :], dsum[:, t, :], ACT.Ln, scale=4.0, bias=b["fifth"])
 
-        def squash(rows, b):
-            nc.scalar.activation(th[:, rows, :], arg[:, rows, :], ACT.Tanh, bias=b["fifth"])
-            nc.scalar.activation(rden[:, rows, :], lden[:, rows, :], ACT.Sigmoid, scale=-1.0, bias=b["zero"])
-            nc.scalar.activation(sg[:, rows, :], th[:, rows, :], ACT.Sigmoid, scale=-1.0, bias=b["half"])
+        def invert(t, b):
+            nc.scalar.activation(rden[:, t, :], lden[:, t, :], ACT.Sigmoid, scale=-1.0, bias=b["zero"])
+
+        def squash(tiles, b):
+            for t in tiles:
+                nc.scalar.activation(th[:, t, :], arg[:, t, :], ACT.Tanh, bias=b["fifth"])
+            for t in tiles:
+                nc.scalar.activation(sg[:, t, :], th[:, t, :], ACT.Sigmoid, scale=-1.0, bias=b["half"])
+
+        def argument(t):
+            nc.vector.tensor_tensor(arg[:, t, :], dsum[:, t, :], inhb[t // 2][:, t % 2, :], ALU.subtract)
 
         def scale_rows(t):
             nc.vector.scalar_tensor_tensor(share[:, t, :], rden[:, t, :], neg4u[:, t : t + 1], trig[:, t, :], ALU.mult, ALU.mult)
-            nc.vector.tensor_scalar(inhu[:, t, :], inhb[:, t, :], u04[:, t : t + 1], None, ALU.mult)
+            nc.vector.tensor_scalar(inhu[:, t, :], inhb[t // 2][:, t % 2, :], u04[:, t : t + 1], None, ALU.mult)
 
         def log_lam(rows, cols, b):
             nc.scalar.activation(nll[:, rows, cols], sg[:, rows, cols], ACT.Ln, scale=2.0, bias=b["zero"])
@@ -180,28 +200,36 @@ def tile_picked_ylearnh_br_p_kernel(
 
         def finish(rows, cols):
             nc.vector.tensor_tensor(
-                hb[:, cols, rows].rearrange("p (c i) t -> p c t i", i=4),
-                prod[:, rows, cols].rearrange("p t (c i) -> p c t i", i=4),
-                inhu[:, rows, cols].rearrange("p t (c i) -> p c t i", i=4),
+                hb[:, cols, rows],
+                prod[:, rows, cols].rearrange("p t j -> p j t"),
+                inhu[:, rows, cols].rearrange("p t j -> p j t"),
                 ALU.add,
             )
 
         first, second = slice(0, 2), slice(2, 4)
-        every = slice(0, S)
-        chunks = [slice(c, c + CHUNK) for c in range(0, S, CHUNK)]
+        chunks = [slice(0, 256), slice(256, 384), slice(384, 512)]
 
         for t in (0, 1):
             excite(t)
-            log_den(t, b)
-        nc.vector.tensor_tensor(arg[:, first, :], dsum[:, first, :], inhb[:, first, :], ALU.subtract)
-        squash(first, phase_biases(2))
+            argument(t)
+        log_den(0, b)
+        b = phase_biases(2)
+        invert(0, b)
+        squash((0, 1), b)
         b = phase_biases(3)
+        log_den(1, b)
+        log_lam(first, every, b)
         for t in (2, 3):
             excite(t)
             log_den(t, b)
-        nc.vector.tensor_tensor(arg[:, second, :], dsum[:, second, :], inhb[:, second, :], ALU.subtract)
-        log_lam(first, every, b)
-        squash(second, phase_biases(4))
+        inhb.append(keep.tile([P, 2, S], F32, name="inhb1", tag="late"))
+        for t in (2, 3):
+            inhibit(t)
+            argument(t)
+        b = phase_biases(4)
+        for t in (1, 2, 3):
+            invert(t, b)
+        squash((2, 3), b)
         for t in (0, 1):
             scale_rows(t)
         multiply(first, every)
@@ -218,7 +246,7 @@ def tile_picked_ylearnh_br_p_kernel(
         for c, cols in enumerate(chunks):
             nc.vector.quantize_mx(out=hq[:, cols].bitcast(FP8X4), scales=hs[:, cols], in_=hb[:, cols, :].rearrange("p j t -> p (j t)"))
         for c, cols in enumerate(chunks):
-            ob = psum.tile([P, N // P, CHUNK], F32, name="ob%d" % c, tag="zb%d" % c)
+            ob = psum.tile([P, N // P, cols.stop - cols.start], F32, name="ob%d" % c, tag="zb%d" % c)
             for m in range(N // P):
                 nc.tensor.matmul_mx(
                     out=ob[:, m, :],
@@ -229,6 +257,6 @@ def tile_picked_ylearnh_br_p_kernel(
                     start=True,
                     stop=True,
                 )
-            res = sb("res%d" % c, [P, N // P, CHUNK])
+            res = sb("res%d" % c, [P, N // P, cols.stop - cols.start])
             nc.scalar.copy(res[:], ob[:])
             nc.sync.dma_start(out=out[:, cols].rearrange("(m p) j -> p m j", p=P), in_=res[:])

@@ -62,8 +62,8 @@ def tile_picked_ylearnh_br_p_kernel(
 
         nc.sync.dma_start(out=offs_t[:], in_=offs)
         nc.sync.dma_start(out=w2w[:].bitcast(I32), in_=w2_words[0].bitcast(I32))
-        nc.scalar.dma_start(out=xw[:], in_=x_words[0].rearrange("p n t -> p (n t)").bitcast(I32))
         load_scales(nc.sync, xs, x_scales)
+        nc.sync.dma_start(out=xw[:], in_=x_words[0].rearrange("p n t -> p (n t)").bitcast(I32))
         load_scales(nc.sync, w2s, w2_scales)
         nc.sync.dma_start(out=w1w[:].bitcast(I32), in_=w1_words[0].bitcast(I32))
         load_scales(nc.sync, w1s, w1_scales)
@@ -80,29 +80,31 @@ def tile_picked_ylearnh_br_p_kernel(
         w1d, w2d = sb("w1d", [P, 2 * H], U8), sb("w2d", [P, 2 * H], U8)
         w1sd, w2sd = sb("w1sd", [P, H], U8), sb("w2sd", [P, H], U8)
 
-        def deal_words(dst, src):
+        def deal_words(dst, src, tiles):
             nc.vector.tensor_copy(
-                out=dst[:].rearrange("p (t m b) -> p t m b", t=PACK, b=2),
-                in_=src[:].rearrange("p (m t b) -> p t m b", t=PACK, b=2),
+                out=dst[:].bitcast(U16).rearrange("p (t m) -> p t m", t=PACK)[:, tiles],
+                in_=src[:].bitcast(U16).rearrange("p (m t) -> p t m", t=PACK)[:, tiles],
             )
 
-        def deal_scales(dst, src):
-            nc.vector.tensor_copy(out=dst[:].rearrange("p (t m) -> p t m", t=PACK), in_=src[:].rearrange("p (m t) -> p t m", t=PACK))
+        def deal_scales(dst, src, tiles):
+            nc.vector.tensor_copy(
+                out=dst[:].rearrange("p (t m) -> p t m", t=PACK)[:, tiles], in_=src[:].rearrange("p (m t) -> p t m", t=PACK)[:, tiles]
+            )
 
-        halves = [slice(0, S // 2), slice(S // 2, S)]
         every = slice(0, S)
-
-        def pick(cols):
-            entries = offs_t[:, cols.start // 16 : cols.stop // 16]
-            nc.vector.tensor_copy(out=xgs[:, cols], in_=xs[:].indirect(entries))
-            nc.vector.tensor_copy(out=xg[:, cols], in_=xw[:].bitcast(U32).indirect(entries))
-
-        deal_words(w2d, w2w)
-        pick(halves[0])
-        deal_scales(w2sd, w2s)
-        pick(halves[1])
-        deal_words(w1d, w1w)
-        deal_scales(w1sd, w1s)
+        deal_words(w2d, w2w, slice(0, 2))
+        nc.vector.tensor_copy(out=xgs[:], in_=xs[:].indirect(offs_t[:]))
+        deal_scales(w2sd, w2s, slice(0, 2))
+        halves = [slice(0, S // 2), slice(S // 2, S)]
+        for cols in halves:
+            nc.vector.tensor_copy(out=xg[:, cols], in_=xw[:].bitcast(U32).indirect(offs_t[:, cols.start // 16 : cols.stop // 16]))
+        for words, raw_words, scales, raw_scales, tiles in (
+            (w2d, w2w, w2sd, w2s, slice(2, 4)),
+            (w1d, w1w, w1sd, w1s, slice(0, 2)),
+            (w1d, w1w, w1sd, w1s, slice(2, 4)),
+        ):
+            deal_words(words, raw_words, tiles)
+            deal_scales(scales, raw_scales, tiles)
 
         def product(bank, words, scales, t, cols):
             nc.tensor.matmul_mx(
@@ -122,75 +124,92 @@ def tile_picked_ylearnh_br_p_kernel(
         nc.gpsimd.tensor_scalar(neg4u[:], unit_t[:], -4.0, 0.0, ALU.mult, ALU.add)
         nc.gpsimd.tensor_scalar(u04[:], unit_t[:], 0.4, 0.0, ALU.mult, ALU.add)
 
+        def columns(tile):
+            return {"zero": tile[:, 0:1], "tiny": tile[:, 1:2], "fifth": tile[:, 2:3], "half": tile[:, 3:4]}
+
         def phase_biases(n):
             biases = keep.tile([P, 4], F32, name="biases%d" % n, tag="biases")
             if n == 0:
                 nc.gpsimd.tensor_copy(biases[:], consts[:])
             else:
                 nc.scalar.copy(biases[:], consts[:])
-            return {"zero": biases[:, 0:1], "tiny": biases[:, 1:2], "fifth": biases[:, 2:3], "half": biases[:, 3:4]}
+            return columns(biases)
 
+        free = columns(consts)
         warm = sb("warm", [P, 1])
         nc.scalar.activation(warm[:], consts[:, 0:1], ACT.Sigmoid)
         b = phase_biases(0)
         sz, sy = sb("sz", [P, PACK, S]), sb("sy", [P, PACK, S])
         nz, ny = sb("nz", [P, PACK, S]), sb("ny", [P, PACK, S])
+
+        def sigmoid_of(dst, banks, words, scales, t, cols, b):
+            product(banks[t], words, scales, t, cols)
+            nc.scalar.activation(dst[:, t, cols], banks[t][:, cols], ACT.Sigmoid, scale=-1.0, bias=b["zero"])
+
         for cols in halves:
-            for t in range(PACK):
-                product(zb[t], w2d, w2sd, t, cols)
-                nc.scalar.activation(sz[:, t, cols], zb[t][:, cols], ACT.Sigmoid, scale=-1.0, bias=b["zero"])
-        for t in range(PACK):
-            product(yb[t], w1d, w1sd, t, every)
-            nc.scalar.activation(sy[:, t, :], yb[t][:], ACT.Sigmoid, scale=-1.0, bias=b["zero"])
+            for t in (0, 1):
+                sigmoid_of(sz, zb, w2d, w2sd, t, cols, b)
+        for t in (2, 3):
+            sigmoid_of(sz, zb, w2d, w2sd, t, every, b)
+        for t in (0, 1, 2):
+            sigmoid_of(sy, yb, w1d, w1sd, t, every, b)
+        b = phase_biases(1)
+        sigmoid_of(sy, yb, w1d, w1sd, 3, every, free)
 
         trig = sb("trig", [P, PACK, S])
-        inhb = [sb("inhb0", [P, 2, S])]
-        soft = [sb("soft0", [P, 2, S]), keep.tile([P, 2, S], F32, name="soft1", tag="late")]
+        def shared(name, tag, shape):
+            return keep.tile(shape, F32, name=name, tag=tag, align_bytes=64)
+
+        inhb = [sb("inhb%d" % t, [P, S]) for t in range(3)]
+        soft01 = shared("soft01", "a", [P, 2, S])
+        soft = [soft01[:, 0, :], soft01[:, 1, :], sb("soft2", [P, S])[:], shared("soft3", "b", [P, S])[:]]
+        dsum01, dsum23 = shared("dsum01", "c", [P, 2, S]), sb("dsum23", [P, 2, S])
+        dsum = [dsum01[:, 0, :], dsum01[:, 1, :], dsum23[:, 0, :], dsum23[:, 1, :]]
+        inhu = []
 
         def inhibit(t):
-            nc.vector.tensor_tensor(inhb[t // 2][:, t % 2, :], zw[t][:].indirect(sib_t[:]), inh_t[:, t, :], ALU.mult)
+            nc.vector.tensor_tensor(inhb[t][:], zw[t][:].indirect(sib_t[:]), inh_t[:, t, :], ALU.mult)
 
         for t in range(PACK):
             nc.vector.tensor_copy(out=zw[t][:, :S], in_=zb[t][:])
-        for t in (0, 1):
+        for t in (0, 1, 2):
             inhibit(t)
 
-        b = phase_biases(1)
         for t in range(PACK):
             nc.scalar.activation(nz[:, t, :], sz[:, t, :], ACT.Ln, bias=b["tiny"])
             nc.scalar.activation(ny[:, t, :], sy[:, t, :], ACT.Ln, bias=b["tiny"])
 
-        dsum, arg = sb("dsum", [P, PACK, S]), sb("arg", [P, PACK, S])
+        arg = sb("arg", [P, PACK, S])
         lden, rden = sb("lden", [P, PACK, S]), sb("rden", [P, PACK, S])
         th, sg, nll = sb("th", [P, PACK, S]), sb("sg", [P, PACK, S]), sb("nll", [P, PACK, S])
-        share, inhu, prod = sb("share", [P, PACK, S]), sb("inhu", [P, PACK, S]), sb("prod", [P, PACK, S])
+        share, prod = sb("share", [P, PACK, S]), sb("prod", [P, PACK, S])
         hb = sb("hb", [P, S, PACK], BF16)
         hq, hs = sb("hq", [P, S], U32), sb("hs", [P, S], U8)
 
         def excite(t):
             nc.vector.scalar_tensor_tensor(exc[t][:, :S], nz[:, t, :], -1.0, zb[t][:], ALU.mult, ALU.max)
-            nc.vector.scalar_tensor_tensor(soft[t // 2][:, t % 2, :], ny[:, t, :], -1.0, yb[t][:], ALU.mult, ALU.max)
+            nc.vector.scalar_tensor_tensor(soft[t], ny[:, t, :], -1.0, yb[t][:], ALU.mult, ALU.max)
             nc.vector.tensor_tensor(trig[:, t, :], exc[t][:].indirect(par_t[:]), dec_t[:, t, :], ALU.mult)
-            nc.vector.tensor_tensor(dsum[:, t, :], soft[t // 2][:, t % 2, :], trig[:, t, :], ALU.add)
+            nc.vector.tensor_tensor(dsum[t], soft[t], trig[:, t, :], ALU.add)
 
-        def log_den(t, b):
-            nc.scalar.activation(lden[:, t, :], dsum[:, t, :], ACT.Ln, scale=4.0, bias=b["fifth"])
+        def log_den(t, b, cols=every):
+            nc.scalar.activation(lden[:, t, cols], dsum[t][:, cols], ACT.Ln, scale=4.0, bias=b["fifth"])
 
-        def invert(t, b):
-            nc.scalar.activation(rden[:, t, :], lden[:, t, :], ACT.Sigmoid, scale=-1.0, bias=b["zero"])
+        def invert(t, b, cols=every):
+            nc.scalar.activation(rden[:, t, cols], lden[:, t, cols], ACT.Sigmoid, scale=-1.0, bias=b["zero"])
 
-        def squash(tiles, b):
-            for t in tiles:
-                nc.scalar.activation(th[:, t, :], arg[:, t, :], ACT.Tanh, bias=b["fifth"])
-            for t in tiles:
-                nc.scalar.activation(sg[:, t, :], th[:, t, :], ACT.Sigmoid, scale=-1.0, bias=b["half"])
+        def bound(t, b):
+            nc.scalar.activation(th[:, t, :], arg[:, t, :], ACT.Tanh, bias=b["fifth"])
+
+        def squash(rows, cols, b):
+            nc.scalar.activation(sg[:, rows, cols], th[:, rows, cols], ACT.Sigmoid, scale=-1.0, bias=b["half"])
 
         def argument(t):
-            nc.vector.tensor_tensor(arg[:, t, :], dsum[:, t, :], inhb[t // 2][:, t % 2, :], ALU.subtract)
+            nc.vector.tensor_tensor(arg[:, t, :], dsum[t], inhb[t][:], ALU.subtract)
 
         def scale_rows(t):
             nc.vector.scalar_tensor_tensor(share[:, t, :], rden[:, t, :], neg4u[:, t : t + 1], trig[:, t, :], ALU.mult, ALU.mult)
-            nc.vector.tensor_scalar(inhu[:, t, :], inhb[t // 2][:, t % 2, :], u04[:, t : t + 1], None, ALU.mult)
+            nc.vector.tensor_scalar(inhu[t // 2][:, t % 2, :], inhb[t][:], u04[:, t : t + 1], None, ALU.mult)
 
         def log_lam(rows, cols, b):
             nc.scalar.activation(nll[:, rows, cols], sg[:, rows, cols], ACT.Ln, scale=2.0, bias=b["zero"])
@@ -202,43 +221,56 @@ def tile_picked_ylearnh_br_p_kernel(
             nc.vector.tensor_tensor(
                 hb[:, cols, rows],
                 prod[:, rows, cols].rearrange("p t j -> p j t"),
-                inhu[:, rows, cols].rearrange("p t j -> p j t"),
+                inhu[rows.start // 2][:, :, cols].rearrange("p t j -> p j t"),
                 ALU.add,
             )
 
         first, second = slice(0, 2), slice(2, 4)
-        chunks = [slice(0, 256), slice(256, 384), slice(384, 512)]
+        chunks = [slice(0, 128), slice(128, 384), slice(384, 512)]
 
         for t in (0, 1):
             excite(t)
             argument(t)
-        log_den(0, b)
         b = phase_biases(2)
-        invert(0, b)
-        squash((0, 1), b)
+        for cols in halves:
+            log_den(0, free, cols)
+        invert(0, b, halves[0])
+        bound(0, b)
+        invert(0, b, halves[1])
+        bound(1, b)
+        squash(slice(0, 1), every, free)
         b = phase_biases(3)
+        squash(slice(1, 2), every, free)
         log_den(1, b)
         log_lam(first, every, b)
         for t in (2, 3):
             excite(t)
-            log_den(t, b)
-        inhb.append(keep.tile([P, 2, S], F32, name="inhb1", tag="late"))
-        for t in (2, 3):
-            inhibit(t)
-            argument(t)
+        log_den(2, b)
+        for cols in halves:
+            log_den(3, b, cols)
+        argument(2)
+        inhb.append(shared("inhb3", "b", [P, S]))
+        inhibit(3)
+        argument(3)
+        inhu.append(shared("inhu01", "a", [P, 2, S]))
+        inhu.append(shared("inhu23", "c", [P, 2, S]))
+        invert(3, free, halves[0])
         b = phase_biases(4)
-        for t in (1, 2, 3):
-            invert(t, b)
-        squash((2, 3), b)
+        invert(3, free, halves[1])
+        bound(2, b)
+        invert(1, b)
+        bound(3, b)
+        invert(2, b)
+        for cols in chunks:
+            squash(second, cols, free)
         for t in (0, 1):
             scale_rows(t)
         multiply(first, every)
         finish(first, every)
-        for t in (2, 3):
+        for t in (3, 2):
             scale_rows(t)
-        b = phase_biases(5)
         for cols in chunks:
-            log_lam(second, cols, b)
+            log_lam(second, cols, free)
         for cols in chunks:
             multiply(second, cols)
         for cols in chunks:
@@ -246,10 +278,11 @@ def tile_picked_ylearnh_br_p_kernel(
         for c, cols in enumerate(chunks):
             nc.vector.quantize_mx(out=hq[:, cols].bitcast(FP8X4), scales=hs[:, cols], in_=hb[:, cols, :].rearrange("p j t -> p (j t)"))
         for c, cols in enumerate(chunks):
-            ob = psum.tile([P, N // P, cols.stop - cols.start], F32, name="ob%d" % c, tag="zb%d" % c)
-            for m in range(N // P):
+            width = cols.stop - cols.start
+            for m, (banks, copy, queue) in enumerate((("zb", nc.scalar.copy, nc.scalar), ("yb", nc.vector.tensor_copy, nc.sync))):
+                ob = psum.tile([P, width], F32, name="ob%d%d" % (c, m), tag="%s%d" % (banks, c))
                 nc.tensor.matmul_mx(
-                    out=ob[:, m, :],
+                    out=ob[:],
                     lhsT=w3w[:, 2 * P * m : 2 * P * (m + 1)].bitcast(FP4X4),
                     lhsT_scale=w3s[:, P * m : P * (m + 1)],
                     rhs=hq[:, cols].bitcast(FP8X4),
@@ -257,6 +290,8 @@ def tile_picked_ylearnh_br_p_kernel(
                     start=True,
                     stop=True,
                 )
-            res = sb("res%d" % c, [P, N // P, cols.stop - cols.start])
-            nc.scalar.copy(res[:], ob[:])
-            nc.sync.dma_start(out=out[:, cols].rearrange("(m p) j -> p m j", p=P), in_=res[:])
+                res = sb("res%d%d" % (c, m), [P, width])
+                if c < len(chunks) - 1:
+                    copy, queue = nc.scalar.copy, nc.sync
+                copy(res[:], ob[:])
+                queue.dma_start(out=out[P * m : P * (m + 1), cols], in_=res[:])

@@ -156,126 +156,108 @@ def tile_picked_ylearnh_br_p_kernel(
         b = phase_biases(1)
         sigmoid_of(sy, yb, w1d, w1sd, 3, every, free)
 
-        trig = sb("trig", [P, PACK, S])
-        def shared(name, tag, shape):
-            return keep.tile(shape, F32, name=name, tag=tag, align_bytes=64)
-
-        inhb = [sb("inhb%d" % t, [P, S]) for t in range(3)]
-        soft01 = shared("soft01", "a", [P, 2, S])
-        soft = [soft01[:, 0, :], soft01[:, 1, :], sb("soft2", [P, S])[:], shared("soft3", "b", [P, S])[:]]
-        dsum01, dsum23 = shared("dsum01", "c", [P, 2, S]), sb("dsum23", [P, 2, S])
-        dsum = [dsum01[:, 0, :], dsum01[:, 1, :], dsum23[:, 0, :], dsum23[:, 1, :]]
-        inhu = []
-
-        def inhibit(t):
-            nc.vector.tensor_tensor(inhb[t][:], zw[t][:].indirect(sib_t[:]), inh_t[:, t, :], ALU.mult)
-
-        for t in range(PACK):
-            nc.vector.tensor_copy(out=zw[t][:, :S], in_=zb[t][:])
-        for t in (0, 1, 2):
-            inhibit(t)
-
-        for t in range(PACK):
-            nc.scalar.activation(nz[:, t, :], sz[:, t, :], ACT.Ln, bias=b["tiny"])
-            nc.scalar.activation(ny[:, t, :], sy[:, t, :], ACT.Ln, bias=b["tiny"])
-
-        arg = sb("arg", [P, PACK, S])
+        trig, dsum = sb("trig", [P, PACK, S]), sb("dsum", [P, PACK, S])
+        last = PACK - 1
+        inhb = [sb("inhb%d" % t, [P, S])[:] for t in range(last)]
+        soft = [sb("soft%d" % t, [P, S])[:] for t in range(last)]
+        soft.append(keep.tile([P, S], F32, name="soft_last", tag="late", align_bytes=64)[:])
         lden, rden = sb("lden", [P, PACK, S]), sb("rden", [P, PACK, S])
         th, sg, nll = sb("th", [P, PACK, S]), sb("sg", [P, PACK, S]), sb("nll", [P, PACK, S])
         share, prod = sb("share", [P, PACK, S]), sb("prod", [P, PACK, S])
         hb = sb("hb", [P, S, PACK], BF16)
         hq, hs = sb("hq", [P, S], U32), sb("hs", [P, S], U8)
+        parent = [None] + [sb("parent%d" % t, [P, S]) for t in range(1, PACK)]
 
-        def excite(t):
+        def inhibit(t):
+            nc.vector.tensor_tensor(inhb[t], zw[t][:].indirect(sib_t[:]), inh_t[:, t, :], ALU.mult)
+
+        for t in range(PACK):
+            nc.vector.tensor_copy(out=zw[t][:, :S], in_=zb[t][:])
+        for t in range(last):
+            inhibit(t)
+
+        def mark(t):
+            nc.scalar.activation(nz[:, t, :], sz[:, t, :], ACT.Ln, bias=b["tiny"])
             nc.vector.scalar_tensor_tensor(exc[t][:, :S], nz[:, t, :], -1.0, zb[t][:], ALU.mult, ALU.max)
+
+        def base(t):
+            nc.scalar.activation(ny[:, t, :], sy[:, t, :], ACT.Ln, bias=b["tiny"])
             nc.vector.scalar_tensor_tensor(soft[t], ny[:, t, :], -1.0, yb[t][:], ALU.mult, ALU.max)
-            nc.vector.tensor_tensor(trig[:, t, :], exc[t][:].indirect(par_t[:]), dec_t[:, t, :], ALU.mult)
-            nc.vector.tensor_tensor(dsum[t], soft[t], trig[:, t, :], ALU.add)
 
-        def log_den(t, b, cols=every):
-            nc.scalar.activation(lden[:, t, cols], dsum[t][:, cols], ACT.Ln, scale=4.0, bias=b["fifth"])
+        def fetch(t):
+            nc.scalar.activation(parent[t][:], exc[t][:].indirect(par_t[:]), ACT.Copy)
 
-        def invert(t, b, cols=every):
-            nc.scalar.activation(rden[:, t, cols], lden[:, t, cols], ACT.Sigmoid, scale=-1.0, bias=b["zero"])
+        def trigger(t):
+            looked_up = exc[t][:].indirect(par_t[:]) if t == 0 else parent[t][:]
+            nc.vector.tensor_tensor(trig[:, t, :], looked_up, dec_t[:, t, :], ALU.mult)
 
-        def bound(t, b):
-            nc.scalar.activation(th[:, t, :], arg[:, t, :], ACT.Tanh, bias=b["fifth"])
+        def total(t):
+            nc.vector.tensor_tensor(dsum[:, t, :], soft[t], trig[:, t, :], ALU.add)
 
-        def squash(rows, cols, b):
-            nc.scalar.activation(sg[:, rows, cols], th[:, rows, cols], ACT.Sigmoid, scale=-1.0, bias=b["half"])
+        def log_den(t, cols=every):
+            nc.scalar.activation(lden[:, t, cols], dsum[:, t, cols], ACT.Ln, scale=4.0, bias=b["fifth"])
 
-        def argument(t):
-            nc.vector.tensor_tensor(arg[:, t, :], dsum[t], inhb[t][:], ALU.subtract)
+        mark(0)
+        mark(1)
+        trigger(0)
+        base(0)
+        mark(2)
+        total(0)
+        base(1)
+        fetch(1)
+        mark(3)
+        trigger(1)
+        total(1)
+        fetch(2)
+        base(2)
+        trigger(2)
+        total(2)
+        base(3)
+        fetch(3)
+        trigger(3)
+        total(3)
+        for t in range(last):
+            log_den(t)
+        for cols in halves:
+            log_den(last, cols)
 
-        def scale_rows(t):
+        late = keep.tile([P, 2 * PACK + 1, S], F32, name="late", tag="late", align_bytes=64)
+        arg, inhu = late[:, :PACK, :], late[:, PACK : 2 * PACK, :]
+        inhb.append(late[:, 2 * PACK, :])
+        for t in range(PACK):
+            if t == last:
+                inhibit(t)
+            nc.vector.tensor_tensor(arg[:, t, :], dsum[:, t, :], inhb[t], ALU.subtract)
+
+        def invert(t, biases, cols=every):
+            nc.scalar.activation(rden[:, t, cols], lden[:, t, cols], ACT.Sigmoid, scale=-1.0, bias=biases["zero"])
+
+        def bound(t):
+            nc.scalar.activation(th[:, t, :], arg[:, t, :], ACT.Tanh, bias=free["fifth"])
+
+        invert(last, free, halves[0])
+        b = phase_biases(2)
+        invert(last, free, halves[1])
+        bound(0)
+        for t in range(last):
+            bound(t + 1)
+            invert(t, b)
+        chunks = [slice(c, c + P) for c in range(0, S, P)]
+        for cols in chunks:
+            nc.scalar.activation(sg[:, :, cols], th[:, :, cols], ACT.Sigmoid, scale=-1.0, bias=free["half"])
+        for t in (last, 0, 1, 2):
+            nc.vector.tensor_scalar(inhu[:, t, :], inhb[t], u04[:, t : t + 1], None, ALU.mult)
             nc.vector.scalar_tensor_tensor(share[:, t, :], rden[:, t, :], neg4u[:, t : t + 1], trig[:, t, :], ALU.mult, ALU.mult)
-            nc.vector.tensor_scalar(inhu[t // 2][:, t % 2, :], inhb[t][:], u04[:, t : t + 1], None, ALU.mult)
-
-        def log_lam(rows, cols, b):
-            nc.scalar.activation(nll[:, rows, cols], sg[:, rows, cols], ACT.Ln, scale=2.0, bias=b["zero"])
-
-        def multiply(rows, cols):
-            nc.vector.tensor_tensor(prod[:, rows, cols], share[:, rows, cols], nll[:, rows, cols], ALU.mult)
-
-        def finish(rows, cols):
+        for cols in chunks:
+            nc.scalar.activation(nll[:, :, cols], sg[:, :, cols], ACT.Ln, scale=2.0, bias=free["zero"])
+        for cols in chunks:
+            nc.vector.tensor_tensor(prod[:, :, cols], share[:, :, cols], nll[:, :, cols], ALU.mult)
             nc.vector.tensor_tensor(
-                hb[:, cols, rows],
-                prod[:, rows, cols].rearrange("p t j -> p j t"),
-                inhu[rows.start // 2][:, :, cols].rearrange("p t j -> p j t"),
+                hb[:, cols, :].rearrange("p (c i) t -> p c t i", i=4),
+                prod[:, :, cols].rearrange("p t (c i) -> p c t i", i=4),
+                inhu[:, :, cols].rearrange("p t (c i) -> p c t i", i=4),
                 ALU.add,
             )
-
-        first, second = slice(0, 2), slice(2, 4)
-        chunks = [slice(0, 128), slice(128, 384), slice(384, 512)]
-
-        for t in (0, 1):
-            excite(t)
-            argument(t)
-        b = phase_biases(2)
-        for cols in halves:
-            log_den(0, free, cols)
-        invert(0, b, halves[0])
-        bound(0, b)
-        invert(0, b, halves[1])
-        bound(1, b)
-        squash(slice(0, 1), every, free)
-        b = phase_biases(3)
-        squash(slice(1, 2), every, free)
-        log_den(1, b)
-        log_lam(first, every, b)
-        for t in (2, 3):
-            excite(t)
-        log_den(2, b)
-        for cols in halves:
-            log_den(3, b, cols)
-        argument(2)
-        inhb.append(shared("inhb3", "b", [P, S]))
-        inhibit(3)
-        argument(3)
-        inhu.append(shared("inhu01", "a", [P, 2, S]))
-        inhu.append(shared("inhu23", "c", [P, 2, S]))
-        invert(3, free, halves[0])
-        b = phase_biases(4)
-        invert(3, free, halves[1])
-        bound(2, b)
-        invert(1, b)
-        bound(3, b)
-        invert(2, b)
-        for cols in chunks:
-            squash(second, cols, free)
-        for t in (0, 1):
-            scale_rows(t)
-        multiply(first, every)
-        finish(first, every)
-        for t in (3, 2):
-            scale_rows(t)
-        for cols in chunks:
-            log_lam(second, cols, free)
-        for cols in chunks:
-            multiply(second, cols)
-        for cols in chunks:
-            finish(second, cols)
-        for c, cols in enumerate(chunks):
             nc.vector.quantize_mx(out=hq[:, cols].bitcast(FP8X4), scales=hs[:, cols], in_=hb[:, cols, :].rearrange("p j t -> p (j t)"))
         for c, cols in enumerate(chunks):
             width = cols.stop - cols.start

@@ -19,8 +19,12 @@ ACT = mybir.ActivationFunctionType
 
 P = 128
 PACK = 4
+LAST = PACK - 1
 SPARE = 32
-TINY = 2.0 ** -46
+TINY = 2.0**-46
+RUN = 4
+BY_TABLE = slice(0, 128)
+BY_DIVIDER = slice(128, S)
 
 
 def tile_picked_ylearnh_br_p_kernel(
@@ -34,81 +38,100 @@ def tile_picked_ylearnh_br_p_kernel(
         def sb(name, shape, dtype=F32):
             return keep.tile(shape, dtype, name=name, align_bytes=64)
 
-        def load_scales(queue, plane, scales):
-            for q in range(4):
-                queue.dma_start(out=plane[32 * q : 32 * q + 4, :].bitcast(I32), in_=scales[0, 4 * q : 4 * q + 4, :].bitcast(I32))
+        def row_tiles(name):
+            return sb(name, [P, PACK, S])
+
+        every = slice(0, S)
+        halves = [slice(0, S // 2), slice(S // 2, S)]
+        chunks = [slice(c, c + P) for c in range(0, S, P)]
+        low, high = slice(0, PACK // 2), slice(PACK // 2, PACK)
 
         offs_t = keep.tile([P, S // 16], U16, name="offs_t")
         par_t = keep.tile([P, S // 16], U16, name="par_t")
         sib_t = keep.tile([P, S // 16], U16, name="sib_t")
-        xw = sb("xw", [P, T], I32)
-        xs = sb("xs", [P, T], U8)
+        xw, xs = sb("xw", [P, T], I32), sb("xs", [P, T], U8)
         w1w, w2w, w3w = sb("w1w", [P, 2 * H], U8), sb("w2w", [P, 2 * H], U8), sb("w3w", [P, 2 * N], U8)
         w1s, w2s, w3s = sb("w1s", [P, H], U8), sb("w2s", [P, H], U8), sb("w3s", [P, N], U8)
-        dec_t, inh_t = sb("dec_t", [P, PACK, S]), sb("inh_t", [P, PACK, S])
+        dec_t, inh_t = row_tiles("dec_t"), row_tiles("inh_t")
         unit_t = sb("unit_t", [P, PACK])
-        zw = [sb("zw%d" % t, [P, S + SPARE]) for t in range(PACK)]
-        exc = [sb("exc%d" % t, [P, S + SPARE]) for t in range(PACK)]
+        zz1_window = [sb("zz1_window%d" % t, [P, S + SPARE]) for t in range(PACK)]
+        exc_window = [sb("exc_window%d" % t, [P, S + SPARE]) for t in range(PACK)]
 
-        for plane in (xs, w2s, w1s, w3s):
-            nc.gpsimd.memset(plane[:].bitcast(I32), 0)
+        for scale_tile in (xs, w2s, w1s, w3s):
+            nc.gpsimd.memset(scale_tile[:].bitcast(I32), 0)
         consts = sb("consts", [P, 4])
         nc.gpsimd.memset(consts[:], 0.0)
-        for col, value in ((1, TINY), (2, 0.2), (3, -math.log(2.0))):
+        for col, value in ((1, -math.log(2.0)), (2, TINY), (3, 0.2)):
             nc.gpsimd.tensor_scalar(consts[:, col : col + 1], consts[:, 0:1], 1.0, value, ALU.mult, ALU.add)
-
-        for window in zw + exc:
+        zero, minus_ln2, fifth = consts[:, 0:1], consts[:, 1:2], consts[:, 3:4]
+        for window in zz1_window + exc_window:
             nc.gpsimd.memset(window[:, S:], 0.0)
+
+        def load_scales(scale_tile, scales):
+            for q in range(4):
+                nc.sync.dma_start(out=scale_tile[32 * q : 32 * q + 4, :].bitcast(I32), in_=scales[0, 4 * q : 4 * q + 4, :].bitcast(I32))
 
         nc.sync.dma_start(out=offs_t[:], in_=offs)
         nc.sync.dma_start(out=w2w[:].bitcast(I32), in_=w2_words[0].bitcast(I32))
-        load_scales(nc.sync, xs, x_scales)
+        load_scales(xs, x_scales)
         nc.sync.dma_start(out=xw[:], in_=x_words[0].rearrange("p n t -> p (n t)").bitcast(I32))
-        load_scales(nc.sync, w2s, w2_scales)
+        load_scales(w2s, w2_scales)
         nc.sync.dma_start(out=w1w[:].bitcast(I32), in_=w1_words[0].bitcast(I32))
-        load_scales(nc.sync, w1s, w1_scales)
+        load_scales(w1s, w1_scales)
         nc.sync.dma_start(out=sib_t[:], in_=sib)
         nc.sync.dma_start(out=inh_t[:], in_=inh.rearrange("(p t) j -> p t j", t=PACK))
         nc.sync.dma_start(out=par_t[:], in_=par)
         nc.sync.dma_start(out=dec_t[:], in_=dec.rearrange("(p t) j -> p t j", t=PACK))
         nc.sync.dma_start(out=unit_t[:], in_=unit.rearrange("(p t) o -> p (t o)", t=PACK))
         nc.sync.dma_start(out=w3w[:].bitcast(I32), in_=w3_words[0].bitcast(I32))
-        load_scales(nc.sync, w3s, w3_scales)
+        load_scales(w3s, w3_scales)
 
-        xg = sb("xg", [P, S], U32)
-        xgs = sb("xgs", [P, S], U8)
+        xg, xgs = sb("xg", [P, S], U32), sb("xgs", [P, S], U8)
         w1d, w2d = sb("w1d", [P, 2 * H], U8), sb("w2d", [P, 2 * H], U8)
         w1sd, w2sd = sb("w1sd", [P, H], U8), sb("w2sd", [P, H], U8)
 
+        def deal(dst, src, tiles):
+            nc.vector.tensor_copy(
+                out=dst.rearrange("p (t m) -> p t m", t=PACK)[:, tiles], in_=src.rearrange("p (m t) -> p t m", t=PACK)[:, tiles]
+            )
+
         def deal_words(dst, src, tiles):
-            nc.vector.tensor_copy(
-                out=dst[:].bitcast(U16).rearrange("p (t m) -> p t m", t=PACK)[:, tiles],
-                in_=src[:].bitcast(U16).rearrange("p (m t) -> p t m", t=PACK)[:, tiles],
-            )
+            deal(dst[:].bitcast(U16), src[:].bitcast(U16), tiles)
 
-        def deal_scales(dst, src, tiles):
-            nc.vector.tensor_copy(
-                out=dst[:].rearrange("p (t m) -> p t m", t=PACK)[:, tiles], in_=src[:].rearrange("p (m t) -> p t m", t=PACK)[:, tiles]
-            )
-
-        every = slice(0, S)
-        deal_words(w2d, w2w, slice(0, 2))
+        deal_words(w2d, w2w, low)
         nc.vector.tensor_copy(out=xgs[:], in_=xs[:].indirect(offs_t[:]))
-        deal_scales(w2sd, w2s, slice(0, 2))
-        halves = [slice(0, S // 2), slice(S // 2, S)]
+        deal(w2sd[:], w2s[:], low)
         for cols in halves:
             nc.vector.tensor_copy(out=xg[:, cols], in_=xw[:].bitcast(U32).indirect(offs_t[:, cols.start // 16 : cols.stop // 16]))
         for words, raw_words, scales, raw_scales, tiles in (
-            (w2d, w2w, w2sd, w2s, slice(2, 4)),
-            (w1d, w1w, w1sd, w1s, slice(0, 2)),
-            (w1d, w1w, w1sd, w1s, slice(2, 4)),
+            (w2d, w2w, w2sd, w2s, high),
+            (w1d, w1w, w1sd, w1s, low),
+            (w1d, w1w, w1sd, w1s, high),
         ):
             deal_words(words, raw_words, tiles)
-            deal_scales(scales, raw_scales, tiles)
+            deal(scales[:], raw_scales[:], tiles)
 
-        def product(bank, words, scales, t, cols):
+        zz1 = [psum.tile([P, S], F32, name="zz1_%d" % t, tag="zz1_%d" % t) for t in range(PACK)]
+        y = [psum.tile([P, S], F32, name="y_%d" % t, tag="y_%d" % t) for t in range(PACK)]
+
+        unit_m4, unit_04 = sb("unit_m4", [P, PACK]), sb("unit_04", [P, PACK])
+        nc.gpsimd.tensor_scalar(unit_m4[:], unit_t[:], -4.0, 0.0, ALU.mult, ALU.add)
+        nc.gpsimd.tensor_scalar(unit_04[:], unit_t[:], 0.4, 0.0, ALU.mult, ALU.add)
+
+        def phase_biases(name, copy, cols):
+            biases = keep.tile([P, cols.stop - cols.start], F32, name=name, tag="biases")
+            copy(biases[:], consts[:, cols])
+            return biases
+
+        warm = sb("warm", [P, 1])
+        nc.scalar.activation(warm[:], zero, ACT.Sigmoid)
+
+        phase1_zero = phase_biases("phase1_biases", nc.gpsimd.tensor_copy, slice(0, 1))[:]
+        sig_z, sig_y, ln_z, ln_y = row_tiles("sig_z"), row_tiles("sig_y"), row_tiles("ln_z"), row_tiles("ln_y")
+
+        def product_sigmoid(dst, banks, words, scales, t, cols, bias):
             nc.tensor.matmul_mx(
-                out=bank[:, cols],
+                out=banks[t][:, cols],
                 lhsT=words[:, 2 * P * t : 2 * P * (t + 1)].bitcast(FP4X4),
                 lhsT_scale=scales[:, P * t : P * (t + 1)],
                 rhs=xg[:, cols].bitcast(FP8X4),
@@ -116,164 +139,128 @@ def tile_picked_ylearnh_br_p_kernel(
                 start=True,
                 stop=True,
             )
-
-        zb = [psum.tile([P, S], F32, name="zb%d" % t, tag="zb%d" % t) for t in range(PACK)]
-        yb = [psum.tile([P, S], F32, name="yb%d" % t, tag="yb%d" % t) for t in range(PACK)]
-
-        neg4u, u04 = sb("neg4u", [P, PACK]), sb("u04", [P, PACK])
-        nc.gpsimd.tensor_scalar(neg4u[:], unit_t[:], -4.0, 0.0, ALU.mult, ALU.add)
-        nc.gpsimd.tensor_scalar(u04[:], unit_t[:], 0.4, 0.0, ALU.mult, ALU.add)
-
-        def columns(tile):
-            return {"zero": tile[:, 0:1], "tiny": tile[:, 1:2], "fifth": tile[:, 2:3], "half": tile[:, 3:4]}
-
-        def phase_biases(n):
-            biases = keep.tile([P, 4], F32, name="biases%d" % n, tag="biases")
-            if n == 0:
-                nc.gpsimd.tensor_copy(biases[:], consts[:])
-            else:
-                nc.scalar.copy(biases[:], consts[:])
-            return columns(biases)
-
-        free = columns(consts)
-        warm = sb("warm", [P, 1])
-        nc.scalar.activation(warm[:], consts[:, 0:1], ACT.Sigmoid)
-        b = phase_biases(0)
-        sz, sy = sb("sz", [P, PACK, S]), sb("sy", [P, PACK, S])
-        nz, ny = sb("nz", [P, PACK, S]), sb("ny", [P, PACK, S])
-
-        def sigmoid_of(dst, banks, words, scales, t, cols, b):
-            product(banks[t], words, scales, t, cols)
-            nc.scalar.activation(dst[:, t, cols], banks[t][:, cols], ACT.Sigmoid, scale=-1.0, bias=b["zero"])
+            nc.scalar.activation(dst[:, t, cols], banks[t][:, cols], ACT.Sigmoid, scale=-1.0, bias=bias)
 
         for cols in halves:
-            for t in (0, 1):
-                sigmoid_of(sz, zb, w2d, w2sd, t, cols, b)
-        for t in (2, 3):
-            sigmoid_of(sz, zb, w2d, w2sd, t, every, b)
-        for t in (0, 1, 2):
-            sigmoid_of(sy, yb, w1d, w1sd, t, every, b)
-        b = phase_biases(1)
-        sigmoid_of(sy, yb, w1d, w1sd, 3, every, free)
+            for t in range(low.start, low.stop):
+                product_sigmoid(sig_z, zz1, w2d, w2sd, t, cols, phase1_zero)
+        for t in range(high.start, high.stop):
+            product_sigmoid(sig_z, zz1, w2d, w2sd, t, every, phase1_zero)
+        for t in range(LAST):
+            product_sigmoid(sig_y, y, w1d, w1sd, t, every, phase1_zero)
+        phase2_biases = phase_biases("phase2_biases", nc.scalar.copy, slice(2, 4))
+        phase2_tiny, phase2_fifth = phase2_biases[:, 0:1], phase2_biases[:, 1:2]
+        product_sigmoid(sig_y, y, w1d, w1sd, LAST, every, zero)
 
-        trig, dsum = sb("trig", [P, PACK, S]), sb("dsum", [P, PACK, S])
-        last = PACK - 1
-        inhb = [sb("inhb%d" % t, [P, S])[:] for t in range(last)]
-        soft = [sb("soft%d" % t, [P, S])[:] for t in range(last)]
-        soft.append(keep.tile([P, S], F32, name="soft_last", tag="late", align_bytes=64)[:])
-        lden, rden = sb("lden", [P, PACK, S]), sb("rden", [P, PACK, S])
-        th, sg, nll = sb("th", [P, PACK, S]), sb("sg", [P, PACK, S]), sb("nll", [P, PACK, S])
-        share, prod = sb("share", [P, PACK, S]), sb("prod", [P, PACK, S])
-        hb = sb("hb", [P, S, PACK], BF16)
-        hq, hs = sb("hq", [P, S], U32), sb("hs", [P, S], U8)
-        parent = [None] + [sb("parent%d" % t, [P, S]) for t in range(1, PACK)]
+        trig, total = row_tiles("trig"), row_tiles("total")
+        inhb = [sb("inhb%d" % t, [P, S])[:] for t in range(LAST)]
+        soft_y = [sb("soft_y%d" % t, [P, S])[:] for t in range(LAST)]
+        soft_y.append(keep.tile([P, S], F32, name="soft_y_last", tag="after_totals", align_bytes=64)[:])
+        ln_den, inv_den4 = row_tiles("ln_den"), row_tiles("inv_den4")
+        th, sig_th, minus_llam = row_tiles("th"), row_tiles("sig_th"), row_tiles("minus_llam")
+        share, excited = row_tiles("share"), row_tiles("excited")
+        hid = sb("hid", [P, S, PACK], BF16)
+        hid_words, hid_scales = sb("hid_words", [P, S], U32), sb("hid_scales", [P, S], U8)
+        ep = {t: sb("ep%d" % t, [P, S]) for t in range(1, PACK)}
 
         def inhibit(t):
-            nc.vector.tensor_tensor(inhb[t], zw[t][:].indirect(sib_t[:]), inh_t[:, t, :], ALU.mult)
+            nc.vector.tensor_tensor(inhb[t], zz1_window[t][:].indirect(sib_t[:]), inh_t[:, t, :], ALU.mult)
 
         for t in range(PACK):
-            nc.vector.tensor_copy(out=zw[t][:, :S], in_=zb[t][:])
-        for t in range(last):
+            nc.vector.tensor_copy(out=zz1_window[t][:, :S], in_=zz1[t][:])
+        for t in range(LAST):
             inhibit(t)
 
-        def mark(t):
-            nc.scalar.activation(nz[:, t, :], sz[:, t, :], ACT.Ln, bias=b["tiny"])
-            nc.vector.scalar_tensor_tensor(exc[t][:, :S], nz[:, t, :], -1.0, zb[t][:], ALU.mult, ALU.max)
+        def softplus(dst, logs, sigmoids, banks, t):
+            nc.scalar.activation(logs[:, t, :], sigmoids[:, t, :], ACT.Ln, bias=phase2_tiny)
+            nc.vector.scalar_tensor_tensor(dst, logs[:, t, :], -1.0, banks[t][:], ALU.mult, ALU.max)
 
-        def base(t):
-            nc.scalar.activation(ny[:, t, :], sy[:, t, :], ACT.Ln, bias=b["tiny"])
-            nc.vector.scalar_tensor_tensor(soft[t], ny[:, t, :], -1.0, yb[t][:], ALU.mult, ALU.max)
+        def excite(t):
+            softplus(exc_window[t][:, :S], ln_z, sig_z, zz1, t)
 
-        def fetch(t):
-            nc.scalar.activation(parent[t][:], exc[t][:].indirect(par_t[:]), ACT.Copy)
+        def trigger(t, cols, parents):
+            nc.vector.tensor_tensor(trig[:, t, cols], parents, dec_t[:, t, cols], ALU.mult)
 
-        def trigger(t):
-            looked_up = exc[t][:].indirect(par_t[:]) if t == 0 else parent[t][:]
-            nc.vector.tensor_tensor(trig[:, t, :], looked_up, dec_t[:, t, :], ALU.mult)
+        def log_den(t, cols):
+            nc.scalar.activation(ln_den[:, t, cols], total[:, t, cols], ACT.Ln, scale=4.0, bias=phase2_fifth)
 
-        def total(t):
-            nc.vector.tensor_tensor(dsum[:, t, :], soft[t], trig[:, t, :], ALU.add)
-
-        def log_den(t, cols=every):
-            nc.scalar.activation(lden[:, t, cols], dsum[:, t, cols], ACT.Ln, scale=4.0, bias=b["fifth"])
-
-        mark(0)
-        mark(1)
-        trigger(0)
-        base(0)
-        mark(2)
-        total(0)
-        base(1)
-        fetch(1)
-        mark(3)
-        trigger(1)
-        total(1)
-        fetch(2)
-        base(2)
-        trigger(2)
-        total(2)
-        base(3)
-        fetch(3)
-        trigger(3)
-        total(3)
-        for t in range(last):
-            log_den(t)
-        for cols in halves:
-            log_den(last, cols)
-
-        late = keep.tile([P, 2 * PACK + 1, S], F32, name="late", tag="late", align_bytes=64)
-        arg, inhu = late[:, :PACK, :], late[:, PACK : 2 * PACK, :]
-        inhb.append(late[:, 2 * PACK, :])
+        excite(0)
+        excite(1)
+        trigger(0, every, exc_window[0][:].indirect(par_t[:]))
         for t in range(PACK):
-            if t == last:
-                inhibit(t)
-            nc.vector.tensor_tensor(arg[:, t, :], dsum[:, t, :], inhb[t], ALU.subtract)
+            parts = (BY_TABLE, BY_DIVIDER) if t == LAST else (every,)
+            softplus(soft_y[t], ln_y, sig_y, y, t)
+            if t in ep:
+                nc.scalar.activation(ep[t][:], exc_window[t][:].indirect(par_t[:]), ACT.Copy)
+            if t + 2 < PACK:
+                excite(t + 2)
+            if t in ep:
+                for cols in parts:
+                    trigger(t, cols, ep[t][:, cols])
+            for cols in parts:
+                nc.vector.tensor_tensor(total[:, t, cols], soft_y[t][:, cols], trig[:, t, cols], ALU.add)
+        for t in range(LAST - 1):
+            log_den(t, every)
+        log_den(LAST, BY_TABLE)
+        log_den(LAST - 1, every)
 
-        def invert(t, biases, cols=every):
-            nc.scalar.activation(rden[:, t, cols], lden[:, t, cols], ACT.Sigmoid, scale=-1.0, bias=biases["zero"])
+        after_totals = keep.tile([P, 2 * PACK + 1, S], F32, name="after_totals", tag="after_totals", align_bytes=64)
+        arg, inhibited = after_totals[:, :PACK, :], after_totals[:, PACK : 2 * PACK, :]
+        inhb.append(after_totals[:, 2 * PACK, :])
+        for t in range(PACK):
+            if t == LAST:
+                inhibit(t)
+            nc.vector.tensor_tensor(arg[:, t, :], total[:, t, :], inhb[t], ALU.subtract)
+        den4 = sb("den4", [P, BY_DIVIDER.stop - BY_DIVIDER.start])
+        nc.vector.tensor_scalar(den4[:], total[:, LAST, BY_DIVIDER], 4.0, 1.2, ALU.mult, ALU.add)
+        nc.vector.reciprocal(inv_den4[:, LAST, BY_DIVIDER], den4[:])
+
+        def invert(t, cols, bias):
+            nc.scalar.activation(inv_den4[:, t, cols], ln_den[:, t, cols], ACT.Sigmoid, scale=-1.0, bias=bias)
 
         def bound(t):
-            nc.scalar.activation(th[:, t, :], arg[:, t, :], ACT.Tanh, bias=free["fifth"])
+            nc.scalar.activation(th[:, t, :], arg[:, t, :], ACT.Tanh, bias=fifth)
 
-        invert(last, free, halves[0])
-        b = phase_biases(2)
-        invert(last, free, halves[1])
+        invert(LAST, BY_TABLE, zero)
+        phase3_zero = phase_biases("phase3_biases", nc.scalar.copy, slice(0, 1))[:]
         bound(0)
-        for t in range(last):
+        for t in range(LAST):
             bound(t + 1)
-            invert(t, b)
-        chunks = [slice(c, c + P) for c in range(0, S, P)]
+            invert(t, every, phase3_zero)
         for cols in chunks:
-            nc.scalar.activation(sg[:, :, cols], th[:, :, cols], ACT.Sigmoid, scale=-1.0, bias=free["half"])
-        for t in (last, 0, 1, 2):
-            nc.vector.tensor_scalar(inhu[:, t, :], inhb[t], u04[:, t : t + 1], None, ALU.mult)
-            nc.vector.scalar_tensor_tensor(share[:, t, :], rden[:, t, :], neg4u[:, t : t + 1], trig[:, t, :], ALU.mult, ALU.mult)
+            nc.scalar.activation(sig_th[:, :, cols], th[:, :, cols], ACT.Sigmoid, scale=-1.0, bias=minus_ln2)
+        for t in range(PACK):
+            nc.vector.tensor_scalar(inhibited[:, t, :], inhb[t], unit_04[:, t : t + 1], None, ALU.mult)
+            nc.vector.scalar_tensor_tensor(share[:, t, :], inv_den4[:, t, :], unit_m4[:, t : t + 1], trig[:, t, :], ALU.mult, ALU.mult)
+
         for cols in chunks:
-            nc.scalar.activation(nll[:, :, cols], sg[:, :, cols], ACT.Ln, scale=2.0, bias=free["zero"])
+            nc.scalar.activation(minus_llam[:, :, cols], sig_th[:, :, cols], ACT.Ln, scale=2.0, bias=zero)
         for cols in chunks:
-            nc.vector.tensor_tensor(prod[:, :, cols], share[:, :, cols], nll[:, :, cols], ALU.mult)
+            nc.vector.tensor_tensor(excited[:, :, cols], share[:, :, cols], minus_llam[:, :, cols], ALU.mult)
             nc.vector.tensor_tensor(
-                hb[:, cols, :].rearrange("p (c i) t -> p c t i", i=4),
-                prod[:, :, cols].rearrange("p t (c i) -> p c t i", i=4),
-                inhu[:, :, cols].rearrange("p t (c i) -> p c t i", i=4),
+                hid[:, cols, :].rearrange("p (c i) t -> p c t i", i=RUN),
+                excited[:, :, cols].rearrange("p t (c i) -> p c t i", i=RUN),
+                inhibited[:, :, cols].rearrange("p t (c i) -> p c t i", i=RUN),
                 ALU.add,
             )
-            nc.vector.quantize_mx(out=hq[:, cols].bitcast(FP8X4), scales=hs[:, cols], in_=hb[:, cols, :].rearrange("p j t -> p (j t)"))
+            nc.vector.quantize_mx(
+                out=hid_words[:, cols].bitcast(FP8X4), scales=hid_scales[:, cols], in_=hid[:, cols, :].rearrange("p j t -> p (j t)")
+            )
         for c, cols in enumerate(chunks):
-            width = cols.stop - cols.start
-            for m, (banks, copy, queue) in enumerate((("zb", nc.scalar.copy, nc.scalar), ("yb", nc.vector.tensor_copy, nc.sync))):
-                ob = psum.tile([P, width], F32, name="ob%d%d" % (c, m), tag="%s%d" % (banks, c))
+            for m, banks in enumerate(("zz1", "y")):
+                copy, queue = nc.scalar.copy, nc.sync
+                if c == len(chunks) - 1:
+                    copy, queue = ((nc.scalar.copy, nc.scalar), (nc.vector.tensor_copy, nc.sync))[m]
+                acc = psum.tile([P, P], F32, name="acc%d_%d" % (c, m), tag="%s_%d" % (banks, c))
                 nc.tensor.matmul_mx(
-                    out=ob[:],
+                    out=acc[:],
                     lhsT=w3w[:, 2 * P * m : 2 * P * (m + 1)].bitcast(FP4X4),
                     lhsT_scale=w3s[:, P * m : P * (m + 1)],
-                    rhs=hq[:, cols].bitcast(FP8X4),
-                    rhs_scale=hs[:, cols],
+                    rhs=hid_words[:, cols].bitcast(FP8X4),
+                    rhs_scale=hid_scales[:, cols],
                     start=True,
                     stop=True,
                 )
-                res = sb("res%d%d" % (c, m), [P, width])
-                if c < len(chunks) - 1:
-                    copy, queue = nc.scalar.copy, nc.sync
-                copy(res[:], ob[:])
-                queue.dma_start(out=out[P * m : P * (m + 1), cols], in_=res[:])
+                result = sb("result%d_%d" % (c, m), [P, P])
+                copy(result[:], acc[:])
+                queue.dma_start(out=out[P * m : P * (m + 1), cols], in_=result[:])

import math
from contextlib import ExitStack

import concourse.mybir as mybir

K, T, S, N, H = 512, 1024, 512, 256, 512
FLOPS = 2 * K * S * H * 2 + 2 * H * S * N

F32 = mybir.dt.float32
BF16 = mybir.dt.bfloat16
I32 = mybir.dt.int32
U32 = mybir.dt.uint32
U16 = mybir.dt.uint16
U8 = mybir.dt.uint8
FP8X4 = mybir.dt.float8_e4m3fn_x4
FP4X4 = mybir.dt.float4_e2m1fn_x4
ALU = mybir.AluOpType
ACT = mybir.ActivationFunctionType

P = 128
PACK = 4
LAST = PACK - 1
SPARE = 32
TINY = 2.0**-46
RUN = 4
BY_TABLE = slice(0, 128)
BY_DIVIDER = slice(128, S)


def tile_picked_ylearnh_br_p_kernel(
    tc, x_words, x_scales, w1_words, w1_scales, w2_words, w2_scales, dec, inh, unit, w3_words, w3_scales, offs, par, sib, out
):
    nc = tc.nc
    with ExitStack() as ctx:
        keep = ctx.enter_context(tc.tile_pool(name="keep", bufs=1))
        psum = ctx.enter_context(tc.psum_pool(name="psum", bufs=1))

        def sb(name, shape, dtype=F32):
            return keep.tile(shape, dtype, name=name, align_bytes=64)

        def row_tiles(name):
            return sb(name, [P, PACK, S])

        every = slice(0, S)
        halves = [slice(0, S // 2), slice(S // 2, S)]
        chunks = [slice(c, c + P) for c in range(0, S, P)]
        low, high = slice(0, PACK // 2), slice(PACK // 2, PACK)

        offs_t = keep.tile([P, S // 16], U16, name="offs_t")
        par_t = keep.tile([P, S // 16], U16, name="par_t")
        sib_t = keep.tile([P, S // 16], U16, name="sib_t")
        xw, xs = sb("xw", [P, T], I32), sb("xs", [P, T], U8)
        w1w, w2w, w3w = sb("w1w", [P, 2 * H], U8), sb("w2w", [P, 2 * H], U8), sb("w3w", [P, 2 * N], U8)
        w1s, w2s, w3s = sb("w1s", [P, H], U8), sb("w2s", [P, H], U8), sb("w3s", [P, N], U8)
        dec_t, inh_t = row_tiles("dec_t"), row_tiles("inh_t")
        unit_t = sb("unit_t", [P, PACK])
        zz1_window = [sb("zz1_window%d" % t, [P, S + SPARE]) for t in range(PACK)]
        exc_window = [sb("exc_window%d" % t, [P, S + SPARE]) for t in range(PACK)]

        for scale_tile in (xs, w2s, w1s, w3s):
            nc.gpsimd.memset(scale_tile[:].bitcast(I32), 0)
        consts = sb("consts", [P, 4])
        nc.gpsimd.memset(consts[:], 0.0)
        for col, value in ((1, -math.log(2.0)), (2, TINY), (3, 0.2)):
            nc.gpsimd.tensor_scalar(consts[:, col : col + 1], consts[:, 0:1], 1.0, value, ALU.mult, ALU.add)
        zero, minus_ln2, fifth = consts[:, 0:1], consts[:, 1:2], consts[:, 3:4]
        for window in zz1_window + exc_window:
            nc.gpsimd.memset(window[:, S:], 0.0)

        def load_scales(scale_tile, scales):
            for q in range(4):
                nc.sync.dma_start(out=scale_tile[32 * q : 32 * q + 4, :].bitcast(I32), in_=scales[0, 4 * q : 4 * q + 4, :].bitcast(I32))

        nc.sync.dma_start(out=offs_t[:], in_=offs)
        nc.sync.dma_start(out=w2w[:].bitcast(I32), in_=w2_words[0].bitcast(I32))
        load_scales(xs, x_scales)
        nc.sync.dma_start(out=xw[:], in_=x_words[0].rearrange("p n t -> p (n t)").bitcast(I32))
        load_scales(w2s, w2_scales)
        nc.sync.dma_start(out=w1w[:].bitcast(I32), in_=w1_words[0].bitcast(I32))
        load_scales(w1s, w1_scales)
        nc.sync.dma_start(out=sib_t[:], in_=sib)
        nc.sync.dma_start(out=inh_t[:], in_=inh.rearrange("(p t) j -> p t j", t=PACK))
        nc.sync.dma_start(out=par_t[:], in_=par)
        nc.sync.dma_start(out=dec_t[:], in_=dec.rearrange("(p t) j -> p t j", t=PACK))
        nc.sync.dma_start(out=unit_t[:], in_=unit.rearrange("(p t) o -> p (t o)", t=PACK))
        nc.sync.dma_start(out=w3w[:].bitcast(I32), in_=w3_words[0].bitcast(I32))
        load_scales(w3s, w3_scales)

        xg, xgs = sb("xg", [P, S], U32), sb("xgs", [P, S], U8)
        w1d, w2d = sb("w1d", [P, 2 * H], U8), sb("w2d", [P, 2 * H], U8)
        w1sd, w2sd = sb("w1sd", [P, H], U8), sb("w2sd", [P, H], U8)

        def deal(dst, src, tiles):
            nc.vector.tensor_copy(
                out=dst.rearrange("p (t m) -> p t m", t=PACK)[:, tiles], in_=src.rearrange("p (m t) -> p t m", t=PACK)[:, tiles]
            )

        def deal_words(dst, src, tiles):
            deal(dst[:].bitcast(U16), src[:].bitcast(U16), tiles)

        deal_words(w2d, w2w, low)
        nc.vector.tensor_copy(out=xgs[:], in_=xs[:].indirect(offs_t[:]))
        deal(w2sd[:], w2s[:], low)
        for cols in halves:
            nc.vector.tensor_copy(out=xg[:, cols], in_=xw[:].bitcast(U32).indirect(offs_t[:, cols.start // 16 : cols.stop // 16]))
        for words, raw_words, scales, raw_scales, tiles in (
            (w2d, w2w, w2sd, w2s, high),
            (w1d, w1w, w1sd, w1s, low),
            (w1d, w1w, w1sd, w1s, high),
        ):
            deal_words(words, raw_words, tiles)
            deal(scales[:], raw_scales[:], tiles)

        zz1 = [psum.tile([P, S], F32, name="zz1_%d" % t, tag="zz1_%d" % t) for t in range(PACK)]
        y = [psum.tile([P, S], F32, name="y_%d" % t, tag="y_%d" % t) for t in range(PACK)]

        unit_m4, unit_04 = sb("unit_m4", [P, PACK]), sb("unit_04", [P, PACK])
        nc.gpsimd.tensor_scalar(unit_m4[:], unit_t[:], -4.0, 0.0, ALU.mult, ALU.add)
        nc.gpsimd.tensor_scalar(unit_04[:], unit_t[:], 0.4, 0.0, ALU.mult, ALU.add)

        def phase_biases(name, copy, cols):
            biases = keep.tile([P, cols.stop - cols.start], F32, name=name, tag="biases")
            copy(biases[:], consts[:, cols])
            return biases

        warm = sb("warm", [P, 1])
        nc.scalar.activation(warm[:], zero, ACT.Sigmoid)

        phase1_zero = phase_biases("phase1_biases", nc.gpsimd.tensor_copy, slice(0, 1))[:]
        sig_z, sig_y, ln_z, ln_y = row_tiles("sig_z"), row_tiles("sig_y"), row_tiles("ln_z"), row_tiles("ln_y")

        def product_sigmoid(dst, banks, words, scales, t, cols, bias):
            nc.tensor.matmul_mx(
                out=banks[t][:, cols],
                lhsT=words[:, 2 * P * t : 2 * P * (t + 1)].bitcast(FP4X4),
                lhsT_scale=scales[:, P * t : P * (t + 1)],
                rhs=xg[:, cols].bitcast(FP8X4),
                rhs_scale=xgs[:, cols],
                start=True,
                stop=True,
            )
            nc.scalar.activation(dst[:, t, cols], banks[t][:, cols], ACT.Sigmoid, scale=-1.0, bias=bias)

        for cols in halves:
            for t in range(low.start, low.stop):
                product_sigmoid(sig_z, zz1, w2d, w2sd, t, cols, phase1_zero)
        for t in range(high.start, high.stop):
            product_sigmoid(sig_z, zz1, w2d, w2sd, t, every, phase1_zero)
        for t in range(LAST):
            product_sigmoid(sig_y, y, w1d, w1sd, t, every, phase1_zero)
        phase2_biases = phase_biases("phase2_biases", nc.scalar.copy, slice(2, 4))
        phase2_tiny, phase2_fifth = phase2_biases[:, 0:1], phase2_biases[:, 1:2]
        product_sigmoid(sig_y, y, w1d, w1sd, LAST, every, zero)

        trig, total = row_tiles("trig"), row_tiles("total")
        inhb = [sb("inhb%d" % t, [P, S])[:] for t in range(LAST)]
        soft_y = [sb("soft_y%d" % t, [P, S])[:] for t in range(LAST)]
        soft_y.append(keep.tile([P, S], F32, name="soft_y_last", tag="after_totals", align_bytes=64)[:])
        ln_den, inv_den4 = row_tiles("ln_den"), row_tiles("inv_den4")
        th, sig_th, minus_llam = row_tiles("th"), row_tiles("sig_th"), row_tiles("minus_llam")
        share, excited = row_tiles("share"), row_tiles("excited")
        hid = sb("hid", [P, S, PACK], BF16)
        hid_words, hid_scales = sb("hid_words", [P, S], U32), sb("hid_scales", [P, S], U8)
        ep = {t: sb("ep%d" % t, [P, S]) for t in range(1, PACK)}

        def inhibit(t):
            nc.vector.tensor_tensor(inhb[t], zz1_window[t][:].indirect(sib_t[:]), inh_t[:, t, :], ALU.mult)

        for t in range(PACK):
            nc.vector.tensor_copy(out=zz1_window[t][:, :S], in_=zz1[t][:])
        for t in range(LAST):
            inhibit(t)

        def softplus(dst, logs, sigmoids, banks, t):
            nc.scalar.activation(logs[:, t, :], sigmoids[:, t, :], ACT.Ln, bias=phase2_tiny)
            nc.vector.scalar_tensor_tensor(dst, logs[:, t, :], -1.0, banks[t][:], ALU.mult, ALU.max)

        def excite(t):
            softplus(exc_window[t][:, :S], ln_z, sig_z, zz1, t)

        def trigger(t, cols, parents):
            nc.vector.tensor_tensor(trig[:, t, cols], parents, dec_t[:, t, cols], ALU.mult)

        def log_den(t, cols):
            nc.scalar.activation(ln_den[:, t, cols], total[:, t, cols], ACT.Ln, scale=4.0, bias=phase2_fifth)

        excite(0)
        excite(1)
        trigger(0, every, exc_window[0][:].indirect(par_t[:]))
        for t in range(PACK):
            parts = (BY_TABLE, BY_DIVIDER) if t == LAST else (every,)
            softplus(soft_y[t], ln_y, sig_y, y, t)
            if t in ep:
                nc.scalar.activation(ep[t][:], exc_window[t][:].indirect(par_t[:]), ACT.Copy)
            if t + 2 < PACK:
                excite(t + 2)
            if t in ep:
                for cols in parts:
                    trigger(t, cols, ep[t][:, cols])
            for cols in parts:
                nc.vector.tensor_tensor(total[:, t, cols], soft_y[t][:, cols], trig[:, t, cols], ALU.add)
        for t in range(LAST - 1):
            log_den(t, every)
        log_den(LAST, BY_TABLE)
        log_den(LAST - 1, every)

        after_totals = keep.tile([P, 2 * PACK + 1, S], F32, name="after_totals", tag="after_totals", align_bytes=64)
        arg, inhibited = after_totals[:, :PACK, :], after_totals[:, PACK : 2 * PACK, :]
        inhb.append(after_totals[:, 2 * PACK, :])
        for t in range(PACK):
            if t == LAST:
                inhibit(t)
            nc.vector.tensor_tensor(arg[:, t, :], total[:, t, :], inhb[t], ALU.subtract)
        den4 = sb("den4", [P, BY_DIVIDER.stop - BY_DIVIDER.start])
        nc.vector.tensor_scalar(den4[:], total[:, LAST, BY_DIVIDER], 4.0, 1.2, ALU.mult, ALU.add)
        nc.vector.reciprocal(inv_den4[:, LAST, BY_DIVIDER], den4[:])

        def invert(t, cols, bias):
            nc.scalar.activation(inv_den4[:, t, cols], ln_den[:, t, cols], ACT.Sigmoid, scale=-1.0, bias=bias)

        def bound(t):
            nc.scalar.activation(th[:, t, :], arg[:, t, :], ACT.Tanh, bias=fifth)

        invert(LAST, BY_TABLE, zero)
        phase3_zero = phase_biases("phase3_biases", nc.scalar.copy, slice(0, 1))[:]
        bound(0)
        for t in range(LAST):
            bound(t + 1)
            invert(t, every, phase3_zero)
        for cols in chunks:
            nc.scalar.activation(sig_th[:, :, cols], th[:, :, cols], ACT.Sigmoid, scale=-1.0, bias=minus_ln2)
        for t in range(PACK):
            nc.vector.tensor_scalar(inhibited[:, t, :], inhb[t], unit_04[:, t : t + 1], None, ALU.mult)
            nc.vector.scalar_tensor_tensor(share[:, t, :], inv_den4[:, t, :], unit_m4[:, t : t + 1], trig[:, t, :], ALU.mult, ALU.mult)

        for cols in chunks:
            nc.scalar.activation(minus_llam[:, :, cols], sig_th[:, :, cols], ACT.Ln, scale=2.0, bias=zero)
        for cols in chunks:
            nc.vector.tensor_tensor(excited[:, :, cols], share[:, :, cols], minus_llam[:, :, cols], ALU.mult)
            nc.vector.tensor_tensor(
                hid[:, cols, :].rearrange("p (c i) t -> p c t i", i=RUN),
                excited[:, :, cols].rearrange("p t (c i) -> p c t i", i=RUN),
                inhibited[:, :, cols].rearrange("p t (c i) -> p c t i", i=RUN),
                ALU.add,
            )
            nc.vector.quantize_mx(
                out=hid_words[:, cols].bitcast(FP8X4), scales=hid_scales[:, cols], in_=hid[:, cols, :].rearrange("p j t -> p (j t)")
            )
        for c, cols in enumerate(chunks):
            for m, banks in enumerate(("zz1", "y")):
                copy, queue = nc.scalar.copy, nc.sync
                if c == len(chunks) - 1:
                    copy, queue = ((nc.scalar.copy, nc.scalar), (nc.vector.tensor_copy, nc.sync))[m]
                acc = psum.tile([P, P], F32, name="acc%d_%d" % (c, m), tag="%s_%d" % (banks, c))
                nc.tensor.matmul_mx(
                    out=acc[:],
                    lhsT=w3w[:, 2 * P * m : 2 * P * (m + 1)].bitcast(FP4X4),
                    lhsT_scale=w3s[:, P * m : P * (m + 1)],
                    rhs=hid_words[:, cols].bitcast(FP8X4),
                    rhs_scale=hid_scales[:, cols],
                    start=True,
                    stop=True,
                )
                result = sb("result%d_%d" % (c, m), [P, P])
                copy(result[:], acc[:])
                queue.dma_start(out=out[P * m : P * (m + 1), cols], in_=result[:])
